import numpy as np, ml_dtypes
CORES = [25,29,65,69,153,157,193,197]
N = 8
import mx_ref
BF = ml_dtypes.bfloat16
def pick(q, e):
    c = np.concatenate([q[0].reshape(128, -1, 4), np.zeros((128, 1, 4), np.uint8)], axis=1); s = np.concatenate([q[1], np.ones((16, 1), np.uint8)], axis=1)
    return (np.ascontiguousarray(c[:, e].reshape(128, -1)), np.ascontiguousarray(s[:, e]))
def join(*qs):
    return (np.concatenate([q[0] for q in qs], axis=1), np.concatenate([q[1] for q in qs], axis=1))
def put(q, e, v):
    c, s = q[0].reshape(128, -1, 4).copy(), q[1].copy(); c[:, e] = v[0].reshape(128, -1, 4); s[:, e] = v[1]
    return (c.reshape(128, -1), s)
def pk(c, s):
    return (np.ascontiguousarray(c), mx_ref.live(s))
def emit(q):
    return q[0], q[1]
def cut(t, i, w=512):
    return t[:, w * i:w * i + w]
def f(rng, *shape):
    return mx_ref.flush((rng.standard_normal(shape, dtype=np.float32) * np.exp2(rng.integers(-2, 3, shape[:-1] + (1,)))).astype(BF))
def wide(rng, *shape, cols=0):
    v = rng.standard_normal(shape, dtype=np.float32) * np.exp2(rng.integers(-12, 13, shape)).astype(np.float32)
    if cols: v *= np.repeat(np.exp2(rng.integers(-cols, cols + 1, shape[:-2] + (1, shape[-1] // 4))) * (rng.random(shape[:-2] + (1, shape[-1] // 4)) > 0.0625), 4, axis=-1).astype(np.float32)
    return mx_ref.flush(v.astype(BF))
P, CAPP, O, L, S = 128, 32, 1, 3, 128
def plain(rng):
    v = np.array(f(rng, 128, 512))
    v[:, 4 * L:] = 0
    return {"x": f(rng, N, 128, 4 * P), "pl": np.stack([v] * N), "w": f(rng, N, 128, 512 * O)}
def sized(rng, *shape):
    return (1 + rng.random(shape)) * rng.choice([-1.0, 1.0], shape)
def planes(rng):
    v = np.zeros((128, 128, 4))
    for b in range(L): v[8 * b:8 * b + 8, b] = sized(rng, 8, 4)
    return np.stack([v.reshape(128, 512)] * N).astype(np.float32).astype(BF)
def aim(v, t, pl):
    for b in range(L):
        g = np.sign(pl[0].astype(np.float32).reshape(128, 128, 4)[8 * b:8 * b + 8, b])
        v[:, 8 * b:8 * b + 8] = np.abs(v[:, 8 * b:8 * b + 8]) * g[None, :, None, :] * (1 - 2 * (t >> b & 1))[:, None, :, None]
    return v.reshape(N, 128, 4 * P).astype(np.float32).astype(BF)
def setup_inputs(rng):
    d = plain(rng)
    v = d["x"].astype(np.float32).reshape(N, 128, P, 4).transpose(1, 0, 2, 3).reshape(128, N * P, 4)
    e, n = rng.permutation(N * P), N * P // 4
    near, of = e[:n], rng.choice(e[n:], n)
    size, change = np.exp2(rng.integers(-1, 2, (n, 1))), rng.choice([0.0, 0.0625, 0.25, 0.5], (n, 1))
    v[:, near] = v[:, of] * size * (1 + change * rng.standard_normal((128, n, 4)))
    d["x"] = mx_ref.flush(v.reshape(128, N, P, 4).transpose(1, 0, 2, 3).reshape(N, 128, 4 * P).astype(BF))
    return d
def setup_inputs_same(rng):
    d, first = plain(rng), rng.permutation(N)
    if first[0] == 0: first[0], first[1] = int(first[1]), int(first[0])
    d["pl"], u = planes(rng), sized(rng, 128, N, 4)
    t = np.stack([rng.permutation(np.flatnonzero(first <= s)[np.arange(P) % (s + 1)]) for s in range(N)])
    v = np.stack([u[:, t[s]] for s in range(N)])
    v[first[0]][:, np.flatnonzero(t[first[0]] == 0)[::2]] = 0
    d["x"] = aim(v, t, d["pl"])
    return d
def setup_inputs_full(rng):
    d, h, r = plain(rng), rng.permutation(N), rng.permutation(N)
    n = rng.integers(CAPP + 1, 2 * CAPP + 1, N)
    n[r[0]] = CAPP
    n[r[1]] = P
    t = np.stack([rng.permutation(np.concatenate([np.full(n[s], h[0]), rng.choice(h[2:], P - n[s])])) for s in range(N)])
    d["pl"] = planes(rng)
    d["x"] = aim(sized(rng, N, 128, P, 4), t, d["pl"])
    return d
def setup_inputs_edge(rng):
    d, n = plain(rng), N * P // 4
    o = np.stack([s * P + rng.permutation(P) for s in range(N)]).reshape(N, P // 4, 4)
    m = np.sort(np.concatenate([rng.permutation(o[:, k].reshape(-1)).reshape(N, 4) for k in range(P // 4)]), axis=1)
    v = np.repeat(rng.choice([-1.0, 1.0], (n, 1, 512)), 4, axis=1)
    e, k = 32 * L + np.argsort(rng.random((n, 512 - 32 * L)), axis=1)[:, :49], np.arange(n)[:, None]
    v[k, 1, e[:, :16]] *= -1
    v[k, 2, e[:, :32]] *= -1
    v[k, 3, e[:, 32:]] *= -1
    x, t = np.zeros((N * P, 512)), np.zeros(N * P, int)
    x[m] = v * np.exp2(rng.integers(0, 2, (n, 1, 1)))
    x[m[0, 3]] = 0
    t[m] = np.repeat(np.arange(P // 4) % N, N)[:, None]
    d["pl"] = planes(rng)
    d["x"] = aim(np.ascontiguousarray(x.reshape(N, P, 128, 4).transpose(0, 2, 1, 3)), t.reshape(N, P), d["pl"])
    return d
def setup_inputs_deal(rng):
    d, t = plain(rng), []
    c = np.ones(N, int)
    c[0], c[N - 1] = 2, 0
    for s in range(N):
        a = np.bincount(rng.permutation(np.repeat(np.arange(N), (CAPP - c[s]) // N))[:P // N - c[s]], minlength=N)
        t.append(rng.permutation(np.repeat(np.arange(N), N * a + c[s])))
    d["pl"] = planes(rng)
    d["x"] = aim(sized(rng, N, 128, P, 4), np.stack(t), d["pl"])
    return d
def setup_inputs_spread(rng):
    d, x = plain(rng), np.array(wide(rng, N, 128, 4 * P, cols=6))
    x[0, :, :4] = -0.0
    d["pl"][:, :, :4] = np.abs(d["pl"][:, :, :4])
    return {**d, "x": x}
def check_inputs(d):
    b = []
    for k in ("x", "pl", "w"):
        v = np.abs(d[k].astype(np.float32))
        if not (np.isfinite(v).all() and ((v == 0) | (v >= 2.0 ** -30) & (v <= 2.0 ** 30)).all()): b.append("a value of " + k)
    v = d["pl"].astype(np.float32)
    if (v[:, :, 4 * L:] != 0).any(): b.append("pl has numbers behind its first L columns")
    if (v != v[:1]).any(): b.append("pl differs between ranks")
    return b
def reference(x, pl, w):
    q = [mx_ref.quantize(np.ascontiguousarray(x[s])) for s in range(N)]
    every = join(*q)
    bucket = []
    for s in range(N):
        z = mx_ref.matmul(mx_ref.quantize(np.ascontiguousarray(pl[s])), q[s])
        bucket.append(sum((z[b] < 0) * 2 ** b for b in range(L)))
    alive = []
    for d in range(N):
        e = np.concatenate([P * s + np.flatnonzero(bucket[s] == d)[:CAPP] for s in range(N)])
        if e.size == 0: continue
        at = np.concatenate([e, np.full(-e.size % 128, -1)])
        m = np.concatenate([mx_ref.matmul(pick(every, at[i:i + 128]), pick(every, at)) for i in range(0, at.size, 128)])
        falls = np.triu(m >= np.float32(0.9375) * np.diagonal(m), 1).any(axis=0)
        alive.append(e[~falls[:e.size]])
    alive = np.concatenate(alive)
    oc, osc = np.zeros((N, 128, 4 * S), np.uint8), np.zeros((N, 16, S), np.uint8)
    num, y = np.zeros((N, 1, S), np.float32), np.zeros((N, 128, O * S), np.float32)
    for r in range(N):
        e = alive[r::N]
        e = np.concatenate([e, np.full(S - e.size, -1)])
        v = pick(every, e)
        oc[r], osc[r] = emit(v)
        num[r, 0] = e
        for o in range(O): y[r, :, o * S:o * S + S] = mx_ref.matmul(mx_ref.quantize(np.ascontiguousarray(cut(w[r], o))), v)
    return {"oc": oc, "osc": osc, "num": num, "y": y}

@@ -1,0 +1,409 @@
+from concourse.bass import DstId, RemoteDMATransfer
+from concourse.mybir import dt, AluOpType, AxisListType, ActivationFunctionType
+
+OP = AluOpType
+COPY = ActivationFunctionType.Copy
+SIGN = ActivationFunctionType.Sign
+X = AxisListType.X
+N, P, L, CAPP = 8, 128, 3, 32
+BIG = 1.0e29
+NV = 9
+NS = 16 - NV
+
+SCRATCH = {}
+for _kind, _list in {
+    "bfloat16": "plh 512 xh 520 wh 512 rstb 384 rst1 512 rst2 2304 one8 8 bits 384 bs 384 mt 1024 cu 1024 cm 1024 su 1024 junk1 1024 "
+                "tt 64 tr 64 bc 256 cum 256 cm2 2304 su2 2304 junk3 1792 cl 64 rm2 1",
+    "float8_e4m3fn_x4": "plc 128 prc 384 xq 130 wq 128 slot1c 256 land1c 256 ccc 256 slot3c 256 land3c 258 fq 128 r1c 64 r3c 64",
+    "uint8": "pls 128 prs 384 xs 130 ws 128 slot1s 256 land1s 256 ccs 256 slot3s 256 land3s 258 fs 128 r1s 64 r3s 64",
+    "uint16": "ofp 24 off1 16 m1 2 nl1 64 offc 16 off3 16 nl3 64 m3 2 offz 8 rm 24",
+    "int32": "pb 4 ni 8 fi 8 jn 8 nn 16 at 96 vi 8 v7 8 xi 8 xsh 8",
+    "float32": "rst9 72 pbf 4 q8 16 q4 8 cc0 256 c32 8 c128 8 rhc 16 rh 16 bi 16 ggc 8 gg 8 k8 2 dm0 128 dm 128 mk 16 ma 8 cp 2 tri 512 "
+               "rc 8 wf 8 acc1 8 offf 16 fl1 8 rr 24 mf 2 ff 8 ft 8 k0 1 eg 4 pd 256 junk2 256 thr 2 xg 512 mx 2 f12 4 nb 256 nt 256 nw 256 "
+               "acc2 7 nwc 256 end 8 n3 256 nt3 256 nm 8 m3f 2 d256 8 it 72 its 72 nf 256 nft 264 no 128 ysb 128",
+}.items():
+    _w = _list.split()
+    for _i in range(0, len(_w), 2):
+        SCRATCH[_w[_i]] = ("sbuf", [128, int(_w[_i + 1])], _kind)
+for _n in ("z0", "z1", "z2", "ga", "gb", "yp"):
+    SCRATCH[_n] = ("psum", [128, 512], "float32")
+SEMAPHORES = ["qv", "qs", "qt", "qp", "ldp", "ldx", "ldw", "ldz", "dout", "ls",
+              "a1", "n1", "c2", "a3", "n3", "rc1", "rs1", "rn1", "rn2", "rc3", "rs3", "rn3"]
+
+
+def wiring(T, topo):
+    cores = T.cores
+    same = [[r for r in range(N) if cores[r] in topo.cores_of(cores[s]) or topo.same_plane(cores[s], cores[r])] for s in range(N)]
+    cross = [[r for r in range(N) if r not in same[s]] for s in range(N)]
+    relays = [[k for k in topo.cores_of(c) if k not in cores and topo.die(k) == topo.die(c)
+               and all(topo.may_write(k, cores[r]) for r in cross[s])][:2] for s, c in enumerate(cores)]
+    return same, cross, relays
+
+
+def eng(topo, src, dst, a, b):
+    return sum(1 << e for e in topo.engines(src, dst)[a:b])
+
+
+def dest(topo, src, dst):
+    rid, pid = topo.addr(dst, src)
+    return DstId(rid=rid, pnc=pid)
+
+
+COL_PEER, COL_FAR, COL_RELAY = 8, 4, 4
+MSG_PEER, MSG_FAR, MSG_RELAY = 4, 8, 8
+
+
+def by8(t, w=32):
+    return w * (4 * (t % 2) + t // 2)
+
+
+def view(T, buf, a, b):
+    v = T[buf][:, a:b]
+    return v.bitcast(dt.uint8) if buf[-1] == "c" else v
+
+
+def relay_program(g, core, T, topo, s, group):
+    to = [T.cores[r] for r in group]
+    sent = [0]
+
+    def go(sem, tr, n):
+        g.wait_ge(T.sem[sem], 4)
+        g.remote_dma_fused(tr, local_sem=T.sem.ls)
+        sent[0] += n
+
+    def cols(sem, buf, land, at, rsem):
+        go(sem, [RemoteDMATransfer(dst_ids=[dest(topo, core, d)], dma_engine_mask=eng(topo, core, d, 4 * i, 4 * i + 4), remote_sem=T.sem[rsem],
+                                   src=view(T, buf, 32 * i, 32 * i + 32), dst=view(T, land, at, at + 32)) for i, d in enumerate(to)], 8)
+
+    def note(sem, src, land, at, rsem):
+        go(sem, [RemoteDMATransfer(dst_ids=[dest(topo, core, d) for d in to], dma_engine_mask=eng(topo, core, to[0], 0, 8), remote_sem=T.sem[rsem],
+                                   srcs=[src], dsts=[T[land][:, at:at + 1]] * 2)], 8)
+
+    cols("rc1", "r1c", "land1c", by8(s), "a1")
+    cols("rs1", "r1s", "land1s", by8(s), "a1")
+    note("rn1", T.rm[:, 0:1], "nl1", by8(s, 8), "n1")
+    note("rn2", T.rm2[:, 0:1], "cl", 8 * s, "c2")
+    cols("rc3", "r3c", "land3c", 32 * s, "a3")
+    cols("rs3", "r3s", "land3s", 32 * s, "a3")
+    note("rn3", T.rm[:, 8:9], "nl3", 8 * s, "n3")
+    g.wait_ge(T.sem.ls, sent[0])
+
+
+def rank_program(g, core, T, topo):
+    same_all, cross_all, relays_all = wiring(T, topo)
+    me = T.rank_of(core)
+    if me is None:
+        for s in range(N):
+            if core in relays_all[s]:
+                i = relays_all[s].index(core)
+                relay_program(g, core, T, topo, s, cross_all[s][2 * i:2 * i + 2])
+        return
+    same, cross, relays = same_all[me], cross_all[me], relays_all[me]
+    pos = cross + same
+    am = same.index(me)
+    peer = [r for r in same if r != me and T.cores[r] in topo.cores_of(core)]
+    far = [r for r in same if r != me and r not in peer]
+    ncol = sum(COL_PEER if r in peer else COL_FAR if r in far else COL_RELAY for r in range(N) if r != me)
+    nmsg = sum(MSG_PEER if r in peer else MSG_FAR if r in far else MSG_RELAY for r in range(N) if r != me)
+
+    V, S, E, Y = g.vector, g.scalar, g.tensor, g.sync
+    Q = {"v": V, "s": S, "t": E, "p": g, "y": Y}
+    cnt, seen = {}, {}
+
+    def wait(q, deps):
+        best = {}
+        for s, v in deps:
+            best[s] = max(best.get(s, 0), v)
+        for s, v in best.items():
+            if seen.get((q, s), 0) < v:
+                Q[q].wait_ge(T.sem[s], v)
+                seen[(q, s)] = v
+
+    def do(q, call, *deps):
+        wait(q, deps)
+        name = "q" + q
+        cnt[name] = cnt.get(name, 0) + 1
+        call().then_inc(T.sem[name], 1)
+        return (name, cnt[name])
+
+    def load(q, sem, out, in_, *deps):
+        wait(q, deps)
+        cnt[sem] = cnt.get(sem, 0) + 16
+        Q[q].dma_start(out, in_).then_inc(T.sem[sem], 16)
+        return (sem, cnt[sem])
+
+    def vset(ap, c, *deps):
+        return do("v", lambda: V.memset(ap, c), *deps)
+
+    def ts(out, in0, s1, s2, op0, op1, *deps):
+        if op1 is None:
+            return do("v", lambda: V.tensor_scalar(out, in0, s1, None, op0), *deps)
+        return do("v", lambda: V.tensor_scalar(out, in0, s1, s2, op0, op1), *deps)
+
+    def tt(out, a, b, op, *deps):
+        return do("v", lambda: V.tensor_tensor(out, a, b, op), *deps)
+
+    def vcopy(out, in_, *deps):
+        return do("v", lambda: V.tensor_copy(out, in_), *deps)
+
+    def red(out, in_, op, *deps):
+        return do("v", lambda: V.tensor_reduce(out, in_, X, op), *deps)
+
+    def scan(out, d0, d1, *deps):
+        return do("v", lambda: V.tensor_tensor_scan(out, d0, d1, 0.0, OP.mult, OP.add), *deps)
+
+    def turn(out, in_, *deps):
+        return do("v", lambda: V.transpose(out, in_), *deps)
+
+    def act(out, in_, *deps):
+        return do("s", lambda: S.activation(out, in_, COPY), *deps)
+
+    def iota(ap, pattern, base, cm=0, flag=True):
+        if flag:
+            return do("p", lambda: g.iota(ap, pattern, base, cm, allow_small_or_imprecise_dtypes=True))
+        return do("p", lambda: g.iota(ap, pattern, base, cm))
+
+    def pickc(out, win, off, *deps):
+        return do("v", lambda: V.tensor_copy(out.bitcast(dt.uint32), win.bitcast(dt.uint32).indirect(off)), *deps)
+
+    def pick(dst, src, n, a, b, off, *deps):
+        return (pickc(T[dst + "c"][:, a:b], T[src[0]][:, 0:n], off, *deps), act(T[dst + "s"][:, a:b], T[src[1]][:, 0:n].indirect(off), *deps))
+
+    def send(tr, *deps):
+        wait("p", deps)
+        g.remote_dma_fused([t for t, n in tr], local_sem=T.sem.ls)
+        cnt["ls"] = cnt.get("ls", 0) + sum(n for t, n in tr)
+
+    def xfer(src, dst, to, a, b, sem):
+        return (RemoteDMATransfer(dst_ids=[dest(topo, core, c) for c in to], dma_engine_mask=eng(topo, core, to[0], a, b), remote_sem=T.sem[sem],
+                                  srcs=[src], dsts=[dst] * len(to)), b - a)
+
+    def send_cross(buf, rbuf, sem, *deps):
+        send([xfer(view(T, buf, 64 * i, 64 * i + 64), view(T, rbuf, 0, 64), [k], 8 + 4 * i, 12 + 4 * i, sem) for i, k in enumerate(relays)], *deps)
+
+    def send_same(buf, land, at, sem, *deps):
+        tr = []
+        for i, r in enumerate(far + peer):
+            a, e = 32 * pos.index(r), (8, 16) if r in peer else (4 * i, 4 * i + 4)
+            tr.append(xfer(view(T, buf, a, a + 32), view(T, land, at, at + 32), [T.cores[r]], e[0], e[1], sem))
+        send(tr, *deps)
+
+    def send_note(to_same, to_cross, land, at, rbuf, sem, rsem, *deps):
+        dst = T[land][:, at:at + 1]
+        send([xfer(to_same, dst, [T.cores[r] for r in far], 0, 8, sem), xfer(to_cross, rbuf, relays, 8, 12, rsem),
+              xfer(to_same, dst, [T.cores[r] for r in peer], 12, 16, sem)], *deps)
+
+    ldp = load("y", "ldp", T.plh[:, 0:16], T.pl[:, 0:16])
+    ldx = load("s", "ldx", T.xh[:, 0:512], T.x[:])
+    ldw = load("y", "ldw", T.wh[:], T.w[:], ldx)
+    i_p = iota(T.pb[:, 0:1], [[1, 1]], 0, 1, False)
+    i_rh = iota(T.rhc[:], [[16, 16]], 0)
+    i_q8 = iota(T.q8[:], [[0, 2], [1, 8]], 0)
+    i_q4 = iota(T.q4[:], [[0, 2], [1, 4]], 0)
+    i_c32 = iota(T.c32[:], [[32, 2], [64, 4]], 256)
+    i_c128 = iota(T.c128[:], [[128, 2], [256, 4]], 0)
+    i_gg = iota(T.ggc[:], [[128, 8]], me)
+    i_cc = iota(T.cc0[:], [[32, 2], [64, 4], [1, 32]], 0)
+    c_pl = vset(T.plh[:, 16:512], 0.0)
+    c_x = vset(T.xh[:, 512:520], 0.0)
+    for b in range(L):
+        c_of = vset(T.ofp[:, 8 * b:8 * b + 8], b)
+    h = vset(T.rstb[:], 1.0)
+    c_rb = vset(T.rstb[:, 0:384:3], 0.0, h)
+    h = vset(T.rst1[:], 1.0)
+    c_r1 = vset(T.rst1[:, 0:512:128], 0.0, h)
+    ts(T.pb[:, 1:2], T.pb[:, 0:1], 15, None, OP.bitwise_and, None, i_p)
+    ts(T.pb[:, 2:3], T.pb[:, 0:1], 4, None, OP.logical_shift_right, None)
+    h = ts(T.pb[:, 3:4], T.pb[:, 0:1], 5, None, OP.logical_shift_right, None)
+    c_pb = vcopy(T.pbf[:], T.pb[:], h)
+    pf, rho, p16, p32 = [T.pbf[:, i:i + 1] for i in range(4)]
+    c_rh = ts(T.rh[:], T.rhc[:], rho, None, OP.add, None, c_pb, i_rh)
+    c_bi = ts(T.bi[:], T.rh[:], 0.5, None, OP.add, None, c_rh)
+
+    h = do("v", lambda: V.quantize_mx(T.plc[:], T.pls[:], T.plh[:]), ldp, c_pl)
+    prc = pickc(T.prc[:], T.plc[:], T.ofp[:], h, c_of)
+    prs = act(T.prs[:], T.pls[:].indirect(T.ofp[:]), h, c_of)
+    xq = do("v", lambda: V.quantize_mx(T.xq[:], T.xs[:], T.xh[:]), ldx, c_x)
+    zs = [T.z0, T.z1, T.z2]
+    for b in range(L):
+        w = slice(128 * b, 128 * b + 128)
+        z = do("t", lambda: E.matmul_mx(zs[b][:, 0:128], T.prc[:, w], T.prs[:, w], T.xq[:, 0:128], T.xs[:, 0:128], True, True), prc, prs, xq)
+        h = ts(T.bits[:, b:384:3], zs[b][:, 0:128], 0.0, float(2 ** b), OP.is_lt, OP.mult, z)
+    bs = scan(T.bs[:], T.rstb[:], T.bits[:], h, c_rb)
+    bucket = T.bs[:, 2:384:3]
+
+    def match(half):
+        for i in range(4 * half, 4 * half + 4):
+            h = ts(T.mt[:, 128 * i:128 * i + 128], bucket, float(pos[i]), None, OP.is_equal, None, bs)
+        return scan(T.cu[:, 512 * half:512 * half + 512], T.rst1[:], T.mt[:, 512 * half:512 * half + 512], h, c_r1)
+
+    def sums_s(half, cu):
+        for i in range(4 * half, 4 * half + 4):
+            w = slice(128 * i, 128 * i + 128)
+            h = do("s", lambda: S.activation(T.junk1[:, w], T.cu[:, w], SIGN, T.bi[:, 1:2], -1.0, accum_out=T.acc1[:, i:i + 1]), cu, c_bi)
+        return h
+
+    def sums_v(half, cu):
+        w = slice(512 * half, 512 * half + 512)
+        h = ts(T.cm[:, w], T.cu[:, w], T.rh[:, 0:1], None, OP.is_le, None, cu)
+        return scan(T.su[:, w], T.rst1[:], T.cm[:, w], h)
+
+    def offsets(half, sv, ss):
+        vcopy(T.off1[:, 8 * half:8 * half + 8:2], T.su[:, 512 * half + 127:512 * half + 512:128], sv)
+        return ts(T.off1[:, 8 * half + 1:8 * half + 8:2], T.acc1[:, 4 * half:4 * half + 4], 0.5, 64.0, OP.mult, OP.add, ss)
+
+    XQ, L1, CC = ("xq", "xs"), ("land1c", "land1s"), ("ccc", "ccs")
+    cu0 = match(0)
+    ss0 = sums_s(0, cu0)
+    sv0 = sums_v(0, cu0)
+    cu1 = match(1)
+    o0 = offsets(0, sv0, ss0)
+    pc, ps = pick("slot1", XQ, 130, 0, 128, T.off1[:, 0:8], o0, xq)
+    send_cross("slot1c", "r1c", "rc1", pc)
+    send_cross("slot1s", "r1s", "rs1", ps)
+    ss1 = sums_s(1, cu1)
+    sv1 = sums_v(1, cu1)
+    c_mk = ts(T.mk[:], T.q8[:], p16, None, OP.is_equal, None, i_q8)
+    for i in range(N):
+        c_wf = vset(T.wf[:, i:i + 1], 256.0 * 2 ** (i % 4))
+    h = ts(T.fl1[:], T.cu[:, 127:1024:128], 4096.0, None, OP.mult, None, cu0, cu1)
+    tt(T.rr[:, 8:16], T.fl1[:], T.wf[:], OP.min, h, c_wf)
+    o1 = offsets(1, sv1, ss1)
+    h = vcopy(T.offf[:], T.off1[:], o1, o0)
+    tt(T.rr[:, 0:8], T.offf[:, 0:8], T.mk[:, 0:8], OP.mult, h, c_mk)
+    h = tt(T.rr[:, 16:24], T.offf[:, 8:16], T.mk[:, 8:16], OP.mult, h)
+    red(T.mf[:, 0:1], T.rr[:, 0:12], OP.add, h)
+    h = red(T.mf[:, 1:2], T.rr[:, 12:24], OP.add, h)
+    m1 = vcopy(T.m1[:], T.mf[:], h)
+    q, q8 = by8(me), by8(me, 8)
+    own_n = vcopy(T.nl1[:, q8:q8 + 1], T.mf[:, 1:2], h)
+    send_note(T.m1[:, 1:2], T.m1[:, 0:1], "nl1", q8, T.rm[:, 0:1], "n1", "rn1", m1)
+    pc, ps = pick("slot1", XQ, 130, 128, 256, T.off1[:, 8:16], o1, xq)
+    send_same("slot1c", "land1c", q, "a1", pc)
+    send_same("slot1s", "land1s", q, "a1", ps)
+    i = pos.index(me)
+    own1 = pick("land1", XQ, 130, q, q + 32, T.off1[:, 2 * i:2 * i + 2], o1, xq)
+
+    load("y", "ldz", T.land3c[:, 256:258].bitcast(dt.uint8), T.xq[:, 128:130].bitcast(dt.uint8), xq)
+    ldz = load("y", "ldz", T.land3s[:, 256:258], T.xs[:, 128:130], xq)
+    h = vset(T.dm0[:], 0.9375)
+    c_dm = do("p", lambda: g.affine_select(T.dm[:], T.dm0[:], [[-1, 128]], OP.is_equal, 0.0, 0, 1), h)
+    h = ts(T.cp[:, 0:1], p32, 32.0, pf, OP.mult, OP.add, c_pb)
+    c_cp = ts(T.cp[:, 1:2], T.cp[:, 0:1], 32.0, None, OP.add, None, h)
+    for b in range(2):
+        c_tri = ts(T.tri[:, 256 * b:256 * b + 256], T.cc0[:], T.cp[:, b:b + 1], -BIG, OP.is_ge, OP.mult, c_cp, i_cc)
+    c_tt = vset(T.tt[:], 0.0)
+    vset(T.nb[:], 0.0)
+    h = vset(T.rst2[:], 1.0)
+    c_r2 = vset(T.rst2[:, 0:NV * 256:256], 0.0, h)
+    h = vset(T.rst9[:], 1.0)
+    vset(T.rst9[:, 0:72:9], 0.0, h)
+    c_one = vset(T.one8[:], 1.0)
+    ts(T.ma[:], T.q4[:], p32, None, OP.is_equal, None, i_q4)
+    h = ts(T.k8[:, 0:1], rho, 8.0, None, OP.mult, None)
+    ts(T.k8[:, 1:2], T.k8[:, 0:1], 128.0, None, OP.add, None, h)
+    c_gg = ts(T.gg[:], T.ggc[:], T.k8[:, 0:1], None, OP.add, None, h, i_gg)
+    vcopy(T.it[:, 0:72:9], T.gg[:], c_gg)
+    for i in range(N):
+        vset(T.rc[:, i:i + 1], 2048.0 + pos[i])
+    vset(T.nf[:], 0.0)
+    vset(T.nft[:, 256:264], -1.0)
+    c_all = do("v", lambda: V.quantize_mx(T.wq[:], T.ws[:], T.wh[:]), ldw)
+
+    a1, n1 = ("a1", 2 * ncol), ("n1", nmsg)
+    ni = vcopy(T.ni[:], T.nl1[:, 0:64:8], n1, own_n)
+    h = ts(T.fi[:], T.ni[:], 8 + am, 1, OP.logical_shift_right, OP.bitwise_and, ni)
+    h = ts(T.ff[:], T.fi[:], -256.0, None, OP.mult, None, h)
+    h = tt(T.ft[:], T.ff[:], T.c32[:], OP.add, h, i_c32)
+    h = red(T.k0[:], T.ft[:], OP.min, h)
+    ts(T.eg[:, 0:2], T.cp[:], T.k0[:, 0:1], None, OP.is_equal, None, h, c_cp)
+    eq = ts(T.eg[:, 2:4], T.cp[:], T.k0[:, 0:1], None, OP.is_ge, None, h)
+    gs, gm, th = [T.ga, T.gb], [], []
+    for b in range(2):
+        w = slice(128 * b, 128 * b + 128)
+        gm.append(do("t", lambda: E.matmul_mx(gs[b][:, 0:256], T.land1c[:, w], T.land1s[:, w], T.land1c[:], T.land1s[:], True, True), a1, *own1))
+    for b in range(2):
+        w = slice(128 * b, 128 * b + 128)
+        h = tt(T.pd[:, w], gs[b][:, w], T.dm[:], OP.mult, gm[b], c_dm)
+        th.append(do("s", lambda: S.activation(T.junk2[:, w], T.pd[:, w], COPY, accum_out=T.thr[:, b:b + 1]), h))
+    for b in range(2):
+        w = slice(256 * b, 256 * b + 256)
+        h = tt(T.xg[:, w], gs[b][:, 0:256], T.tri[:, w], OP.add, c_tri)
+        h = red(T.mx[:, b:b + 1], T.xg[:, w], OP.max, h)
+    h = tt(T.f12[:, 0:2], T.mx[:], T.thr[:], OP.is_lt, h, th[1])
+    h = tt(T.f12[:, 2:4], T.f12[:, 0:2], T.eg[:, 0:2], OP.max, h)
+    h = tt(T.tt[:, 0:64:32], T.f12[:, 2:4], T.eg[:, 2:4], OP.mult, h, eq, c_tt)
+    tr = turn(T.tr[:], T.tt[:], h)
+    for a in range(4):
+        bc = do("p", lambda: g.partition_broadcast(T.bc[:, 64 * a:64 * a + 64], T.tr[32 * a:32 * a + 1, :], 128), tr)
+    h = ts(T.jn[:], T.ni[:], 255, None, OP.bitwise_and, None)
+    h = tt(T.nb[:, 0:256:32], T.jn[:], T.c128[:], OP.add, h, i_c128)
+    nt = turn(T.nt[:], T.nb[:], h)
+    cum = scan(T.cum[:], T.rst2[:, 0:256], T.bc[:], bc, c_r2)
+
+    send_note(T.cum[:, 255:256], T.cum[:, 255:256], "cl", 8 * me, T.rm2[:, 0:1], "c2", "rn2", cum)
+    nw = do("p", lambda: g.partition_broadcast(T.nw[:], T.nt[32 * am:32 * am + 1, :], 128), nt)
+    own_c = vcopy(T.cl[:, 8 * me:8 * me + 1], T.cum[:, 255:256], cum)
+    for c in range(NS):
+        w = slice(256 * c, 256 * c + 256)
+        sa = do("s", lambda: S.activation(T.junk3[:, w], T.cum[:], SIGN, T.bi[:, NV + c:NV + c + 1], -1.0, accum_out=T.acc2[:, c:c + 1]), cum)
+    for c in range(NV):
+        h = ts(T.cm2[:, 256 * c:256 * c + 256], T.cum[:], T.rh[:, c:c + 1], None, OP.is_le, None)
+    h = scan(T.su2[:], T.rst2[:], T.cm2[:], h)
+    vcopy(T.nn[:, 0:NV], T.su2[:, 255:NV * 256:256], h)
+    h = ts(T.nn[:, NV:16], T.acc2[:], 0.5, 128.0, OP.mult, OP.add, sa)
+    t = [T.at[:, 16 * i:16 * i + 16] for i in range(6)]
+    ts(t[0], T.nn[:], 31, None, OP.bitwise_and, None, h)
+    ts(t[1], T.nn[:], 1, 96, OP.logical_shift_right, OP.bitwise_and)
+    h = ts(t[2], T.nn[:], 32, None, OP.bitwise_and, None)
+    tt(t[3], t[0], t[1], OP.add, h)
+    h = ts(t[4], t[2], 4.0, None, OP.mult, None, h)
+    h = tt(t[5], t[3], t[4], OP.add, h)
+    oc = vcopy(T.offc[:], t[5], h)
+    ck = pick("cc", L1, 256, 0, 256, T.offc[:], oc, a1, *own1)
+    nwc = act(T.nwc[:], T.nw[:].indirect(T.offc[:]), oc, nw)
+
+    end = scan(T.end[:], T.one8[:], T.cl[:, 0:64:8], ("c2", nmsg), own_c, c_one)
+    h = ts(T.vi[:], T.rc[:], T.end[:, me - 1:me] if me else 0.0, None, OP.subtract, None, end)
+    h = ts(T.v7[:], T.vi[:], 7, None, OP.bitwise_and, None, h)
+    ts(T.off3[:, 0:16:2], T.v7[:], T.k8[:, 0:1], None, OP.add, None, h)
+    o3 = ts(T.off3[:, 1:16:2], T.v7[:], T.k8[:, 1:2], None, OP.add, None)
+    pc, ps = pick("slot3", CC, 256, 0, 128, T.off3[:, 0:8], o3, *ck)
+    send_cross("slot3c", "r3c", "rc3", pc)
+    send_cross("slot3s", "r3s", "rs3", ps)
+    pc, ps = pick("slot3", CC, 256, 128, 256, T.off3[:, 8:16], o3, *ck)
+    send_same("slot3c", "land3c", 32 * me, "a3", pc)
+    send_same("slot3s", "land3s", 32 * me, "a3", ps)
+    n3 = act(T.n3[:], T.nwc[:].indirect(T.off3[:]), o3, nwc)
+    i = pos.index(me)
+    own3 = pick("land3", CC, 256, 32 * me, 32 * me + 32, T.off3[:, 2 * i:2 * i + 2], o3, *ck)
+    h = turn(T.nt3[:], T.n3[:], n3)
+    h = tt(T.nm[:], T.nt3[:, 0:256:32], T.ma[:], OP.mult, h)
+    red(T.m3f[:, 0:1], T.nm[:, 0:4], OP.add, h)
+    h = red(T.m3f[:, 1:2], T.nm[:, 4:8], OP.add, h)
+    m3 = vcopy(T.m3[:], T.m3f[:], h)
+    own_n3 = vcopy(T.nl3[:, 8 * me:8 * me + 1], T.m3f[:, 1:2], h)
+    send_note(T.m3[:, 1:2], T.m3[:, 0:1], "nl3", 8 * me, T.rm[:, 8:9], "n3", "rn3", m3)
+
+    h = ts(T.d256[:], T.cl[:, 0:64:8], -1.0, 256.0, OP.mult, OP.add)
+    for d in range(N):
+        h2 = ts(T.it[:, 1 + d:72:9], T.gg[:], T.end[:, d:d + 1], T.d256[:, d:d + 1], OP.is_ge, OP.mult, h)
+    h = scan(T.its[:], T.rst9[:], T.it[:], h2)
+    h = vcopy(T.xi[:], T.its[:, 8:72:9], h)
+    h = ts(T.xsh[:], T.xi[:], 3, None, OP.logical_shift_right, None, h)
+    oz = ts(T.offz[:], T.xsh[:], 256.0, None, OP.min, None, h)
+
+    a3 = ("a3", 2 * ncol)
+    fc = pickc(T.fq[:], T.land3c[:], T.offz[:], a3, ldz, oz, *own3)
+    fs = act(T.fs[:], T.land3s[:].indirect(T.offz[:]), a3, ldz, oz, *own3)
+    yp = do("t", lambda: E.matmul_mx(T.yp[:, 0:128], T.wq[:], T.ws[:], T.fq[:], T.fs[:], True, True), fc, fs, c_all)
+    load("y", "dout", T.oc[:], T.fq[:].bitcast(dt.uint8), fc)
+    h = vcopy(T.nf[:, 0:256:32], T.nl3[:, 0:64:8], ("n3", nmsg), own_n3)
+    h = turn(T.nft[:, 0:256], T.nf[:], h)
+    no = do("v", lambda: V.tensor_copy(T.no[:], T.nft[:].indirect(T.offz[:])), h)
+    for k in range(4):
+        load("y", "dout", T.osc[4 * k:4 * k + 4, :], T.fs[32 * k:32 * k + 4, :], fs)
+    ys = act(T.ysb[:], T.yp[:, 0:128], yp)
+    load("s", "dout", T.y[:], T.ysb[:], ys)
+    load("y", "dout", T.num[:], T.no[32 * am:32 * am + 1, :], no)
+    wait("p", [(s, cnt[s]) for s in ("qv", "qs", "qt", "qp", "dout", "ls", "ldz", "ldp", "ldx", "ldw")])

@@ -7,26 +7,26 @@ SIGN = ActivationFunctionType.Sign
 X = AxisListType.X
 N, P, L, CAPP = 8, 128, 3, 32
 BIG = 1.0e29
-NV = 9
-NS = 16 - NV
 
 SCRATCH = {}
 for _kind, _list in {
-    "bfloat16": "plh 512 xh 520 wh 512 rstb 384 rst1 512 rst2 2304 one8 8 bits 384 bs 384 mt 1024 cu 1024 cm 1024 su 1024 junk1 1024 "
-                "tt 64 tr 64 bc 256 cum 256 cm2 2304 su2 2304 junk3 1792 cl 64 rm2 1",
+    "bfloat16": "plh 512 xh 520 wh 512 rstb 384 rst1 256 rst2 512 one 32 bits 384 bs 384 mt 256 cu 256 cm 256 su 256 junk1 256 "
+                "tt 64 cum 256 cm2 512 su2 512 junk3 512 cl 64 rm2 1",
     "float8_e4m3fn_x4": "plc 128 prc 384 xq 130 wq 128 slot1c 256 land1c 256 ccc 256 slot3c 256 land3c 258 fq 128 r1c 64 r3c 64",
     "uint8": "pls 128 prs 384 xs 130 ws 128 slot1s 256 land1s 256 ccs 256 slot3s 256 land3s 258 fs 128 r1s 64 r3s 64",
     "uint16": "ofp 24 off1 16 m1 2 nl1 64 offc 16 off3 16 nl3 64 m3 2 offz 8 rm 24",
-    "int32": "pb 4 ni 8 fi 8 jn 8 nn 16 at 96 vi 8 v7 8 xi 8 xsh 8",
-    "float32": "rst9 72 pbf 4 q8 16 q4 8 cc0 256 c32 8 c128 8 rhc 16 rh 16 bi 16 ggc 8 gg 8 k8 2 dm0 128 dm 128 mk 16 ma 8 cp 2 tri 512 "
-               "rc 8 wf 8 acc1 8 offf 16 fl1 8 rr 24 mf 2 ff 8 ft 8 k0 1 eg 4 pd 256 junk2 256 thr 2 xg 512 mx 2 f12 4 nb 256 nt 256 nw 256 "
-               "acc2 7 nwc 256 end 8 n3 256 nt3 256 nm 8 m3f 2 d256 8 it 72 its 72 nf 256 nft 264 no 128 ysb 128",
+    "int32": "pb 4 ni 8 fi 8 jn 8 vi 8 v7 8 xi 8 xsh 8",
+    "float32": "rst9 72 pbf 4 q4 8 cc0 256 c32 8 c128 8 rhc 4 rh 4 bi 4 rq 4 bq 4 ggc 8 gg 8 k8 2 dm0 128 dm 128 mk 2 ma 8 cp1 1 tri 384 "
+               "rc 8 dq 2 wq2 1 acc1 2 lq 6 la 24 rr 12 mf 6 ff 8 ft 8 k0 1 eg 4 pd 256 junk2 256 thr 2 xg 384 mx 2 f12 4 nb 256 nt 256 "
+               "nw 256 acc2 2 nq 4 na 16 nwc 256 end 8 n3 256 nt3 256 nm 8 m3f 2 d256 8 it 72 its 72 nf 256 nft 264 no 128 ysb 128",
 }.items():
     _w = _list.split()
     for _i in range(0, len(_w), 2):
         SCRATCH[_w[_i]] = ("sbuf", [128, int(_w[_i + 1])], _kind)
 for _n in ("z0", "z1", "z2", "ga", "gb", "yp"):
     SCRATCH[_n] = ("psum", [128, 512], "float32")
+SCRATCH["tw"] = ("sbuf", [128, 2, 32], "bfloat16")
+SCRATCH["bc"] = ("sbuf", [128, 2, 128], "bfloat16")
 SEMAPHORES = ["qv", "qs", "qt", "qp", "ldp", "ldx", "ldw", "ldz", "dout", "ls",
               "a1", "n1", "c2", "a3", "n3", "rc1", "rs1", "rn1", "rn2", "rc3", "rs3", "rn3"]
 
@@ -51,10 +51,7 @@ def dest(topo, src, dst):
 
 COL_PEER, COL_FAR, COL_RELAY = 8, 4, 4
 MSG_PEER, MSG_FAR, MSG_RELAY = 4, 8, 8
-
-
-def by8(t, w=32):
-    return w * (4 * (t % 2) + t // 2)
+HAND = {1: ((8, 12), (12, 16)), 3: ((0, 8), (8, 16))}
 
 
 def view(T, buf, a, b):
@@ -66,26 +63,28 @@ def relay_program(g, core, T, topo, s, group):
     to = [T.cores[r] for r in group]
     sent = [0]
 
-    def go(sem, tr, n):
-        g.wait_ge(T.sem[sem], 4)
+    def go(sem, n, tr):
+        g.wait_ge(T.sem[sem], n)
         g.remote_dma_fused(tr, local_sem=T.sem.ls)
-        sent[0] += n
+        sent[0] += 8
 
-    def cols(sem, buf, land, at, rsem):
-        go(sem, [RemoteDMATransfer(dst_ids=[dest(topo, core, d)], dma_engine_mask=eng(topo, core, d, 4 * i, 4 * i + 4), remote_sem=T.sem[rsem],
-                                   src=view(T, buf, 32 * i, 32 * i + 32), dst=view(T, land, at, at + 32)) for i, d in enumerate(to)], 8)
+    def cols(sem, n, buf, land, rsem):
+        at = 32 * s
+        go(sem, n, [RemoteDMATransfer(dst_ids=[dest(topo, core, d)], dma_engine_mask=eng(topo, core, d, 4 * i, 4 * i + 4), remote_sem=T.sem[rsem],
+                                      src=view(T, buf, 32 * i, 32 * i + 32), dst=view(T, land, at, at + 32)) for i, d in enumerate(to)])
 
-    def note(sem, src, land, at, rsem):
-        go(sem, [RemoteDMATransfer(dst_ids=[dest(topo, core, d) for d in to], dma_engine_mask=eng(topo, core, to[0], 0, 8), remote_sem=T.sem[rsem],
-                                   srcs=[src], dsts=[T[land][:, at:at + 1]] * 2)], 8)
+    def note(sem, src, land, rsem):
+        go(sem, 4, [RemoteDMATransfer(dst_ids=[dest(topo, core, d) for d in to], dma_engine_mask=eng(topo, core, to[0], 0, 8), remote_sem=T.sem[rsem],
+                                      srcs=[src], dsts=[T[land][:, 8 * s:8 * s + 1]] * 2)])
 
-    cols("rc1", "r1c", "land1c", by8(s), "a1")
-    cols("rs1", "r1s", "land1s", by8(s), "a1")
-    note("rn1", T.rm[:, 0:1], "nl1", by8(s, 8), "n1")
-    note("rn2", T.rm2[:, 0:1], "cl", 8 * s, "c2")
-    cols("rc3", "r3c", "land3c", 32 * s, "a3")
-    cols("rs3", "r3s", "land3s", 32 * s, "a3")
-    note("rn3", T.rm[:, 8:9], "nl3", 8 * s, "n3")
+    n1, n3 = [HAND[k][0][1] - HAND[k][0][0] for k in (1, 3)]
+    cols("rc1", n1, "r1c", "land1c", "a1")
+    cols("rs1", n1, "r1s", "land1s", "a1")
+    note("rn1", T.rm[:, 0:1], "nl1", "n1")
+    note("rn2", T.rm2[:, 0:1], "cl", "c2")
+    cols("rc3", n3, "r3c", "land3c", "a3")
+    cols("rs3", n3, "r3s", "land3s", "a3")
+    note("rn3", T.rm[:, 8:9], "nl3", "n3")
     g.wait_ge(T.sem.ls, sent[0])
 
 
@@ -149,8 +148,8 @@ def rank_program(g, core, T, topo):
     def red(out, in_, op, *deps):
         return do("v", lambda: V.tensor_reduce(out, in_, X, op), *deps)
 
-    def scan(out, d0, d1, *deps):
-        return do("v", lambda: V.tensor_tensor_scan(out, d0, d1, 0.0, OP.mult, OP.add), *deps)
+    def scan(out, d0, d1, *deps, init=0.0):
+        return do("v", lambda: V.tensor_tensor_scan(out, d0, d1, init, OP.mult, OP.add), *deps)
 
     def turn(out, in_, *deps):
         return do("v", lambda: V.transpose(out, in_), *deps)
@@ -158,10 +157,26 @@ def rank_program(g, core, T, topo):
     def act(out, in_, *deps):
         return do("s", lambda: S.activation(out, in_, COPY), *deps)
 
+    def count_s(out, junk, in_, bias, *deps):
+        return do("s", lambda: S.activation(junk, in_, SIGN, bias, -1.0, accum_out=out), *deps)
+
     def iota(ap, pattern, base, cm=0, flag=True):
+        last = ("qp", cnt.get("qp", 0))
         if flag:
-            return do("p", lambda: g.iota(ap, pattern, base, cm, allow_small_or_imprecise_dtypes=True))
-        return do("p", lambda: g.iota(ap, pattern, base, cm))
+            return do("p", lambda: g.iota(ap, pattern, base, cm, allow_small_or_imprecise_dtypes=True), last)
+        return do("p", lambda: g.iota(ap, pattern, base, cm), last)
+
+    def quads(out, in_, *deps):
+        for a in range(4):
+            for b in range(4):
+                if b % 2:
+                    hs = act(out(b, a), in_(a), *deps)
+                else:
+                    hv = vcopy(out(b, a), in_(a), *deps)
+        return hv, hs
+
+    def quad(t, a, *cols):
+        return T[t][(slice(32 * a, 32 * a + 32),) + cols]
 
     def pickc(out, win, off, *deps):
         return do("v", lambda: V.tensor_copy(out.bitcast(dt.uint32), win.bitcast(dt.uint32).indirect(off)), *deps)
@@ -178,18 +193,19 @@ def rank_program(g, core, T, topo):
         return (RemoteDMATransfer(dst_ids=[dest(topo, core, c) for c in to], dma_engine_mask=eng(topo, core, to[0], a, b), remote_sem=T.sem[sem],
                                   srcs=[src], dsts=[dst] * len(to)), b - a)
 
-    def send_cross(buf, rbuf, sem, *deps):
-        send([xfer(view(T, buf, 64 * i, 64 * i + 64), view(T, rbuf, 0, 64), [k], 8 + 4 * i, 12 + 4 * i, sem) for i, k in enumerate(relays)], *deps)
+    def send_cross(stage, buf, rbuf, sem, *deps):
+        send([xfer(view(T, buf, 64 * i, 64 * i + 64), view(T, rbuf, 0, 64), [k], HAND[stage][i][0], HAND[stage][i][1], sem)
+              for i, k in enumerate(relays)], *deps)
 
-    def send_same(buf, land, at, sem, *deps):
-        tr = []
+    def send_same(buf, land, sem, *deps):
+        tr, at = [], 32 * me
         for i, r in enumerate(far + peer):
             a, e = 32 * pos.index(r), (8, 16) if r in peer else (4 * i, 4 * i + 4)
             tr.append(xfer(view(T, buf, a, a + 32), view(T, land, at, at + 32), [T.cores[r]], e[0], e[1], sem))
         send(tr, *deps)
 
-    def send_note(to_same, to_cross, land, at, rbuf, sem, rsem, *deps):
-        dst = T[land][:, at:at + 1]
+    def send_note(to_same, to_cross, land, rbuf, sem, rsem, *deps):
+        dst = T[land][:, 8 * me:8 * me + 1]
         send([xfer(to_same, dst, [T.cores[r] for r in far], 0, 8, sem), xfer(to_cross, rbuf, relays, 8, 12, rsem),
               xfer(to_same, dst, [T.cores[r] for r in peer], 12, 16, sem)], *deps)
 
@@ -197,13 +213,18 @@ def rank_program(g, core, T, topo):
     ldx = load("s", "ldx", T.xh[:, 0:512], T.x[:])
     ldw = load("y", "ldw", T.wh[:], T.w[:], ldx)
     i_p = iota(T.pb[:, 0:1], [[1, 1]], 0, 1, False)
-    i_rh = iota(T.rhc[:], [[16, 16]], 0)
-    i_q8 = iota(T.q8[:], [[0, 2], [1, 8]], 0)
+    i_rh = iota(T.rhc[:], [[16, 4]], 0)
+    for a in range(4):
+        for e in range(2):
+            i_dq = iota(quad("dq", a, slice(e, e + 1)), [[0, 1]], pos[4 * e + a])
+    for a in range(4):
+        i_wq = iota(quad("wq2", a, slice(0, 1)), [[0, 1]], 256 * 2 ** a)
+    i_hb = iota(T.mk[:], [[1, 2]], 0)
     i_q4 = iota(T.q4[:], [[0, 2], [1, 4]], 0)
-    i_c32 = iota(T.c32[:], [[32, 2], [64, 4]], 256)
-    i_c128 = iota(T.c128[:], [[128, 2], [256, 4]], 0)
+    i_c32 = iota(T.c32[:], [[32, 8]], 256)
+    i_c128 = iota(T.c128[:], [[128, 8]], 0)
     i_gg = iota(T.ggc[:], [[128, 8]], me)
-    i_cc = iota(T.cc0[:], [[32, 2], [64, 4], [1, 32]], 0)
+    i_cc = iota(T.cc0[:], [[1, 256]], 0)
     c_pl = vset(T.plh[:, 16:512], 0.0)
     c_x = vset(T.xh[:, 512:520], 0.0)
     for b in range(L):
@@ -211,9 +232,9 @@ def rank_program(g, core, T, topo):
     h = vset(T.rstb[:], 1.0)
     c_rb = vset(T.rstb[:, 0:384:3], 0.0, h)
     h = vset(T.rst1[:], 1.0)
-    c_r1 = vset(T.rst1[:, 0:512:128], 0.0, h)
+    c_r1 = vset(T.rst1[:, 0:256:128], 0.0, h)
     ts(T.pb[:, 1:2], T.pb[:, 0:1], 15, None, OP.bitwise_and, None, i_p)
-    ts(T.pb[:, 2:3], T.pb[:, 0:1], 4, None, OP.logical_shift_right, None)
+    ts(T.pb[:, 2:3], T.pb[:, 0:1], 4, 1, OP.logical_shift_right, OP.bitwise_and)
     h = ts(T.pb[:, 3:4], T.pb[:, 0:1], 5, None, OP.logical_shift_right, None)
     c_pb = vcopy(T.pbf[:], T.pb[:], h)
     pf, rho, p16, p32 = [T.pbf[:, i:i + 1] for i in range(4)]
@@ -230,77 +251,65 @@ def rank_program(g, core, T, topo):
         z = do("t", lambda: E.matmul_mx(zs[b][:, 0:128], T.prc[:, w], T.prs[:, w], T.xq[:, 0:128], T.xs[:, 0:128], True, True), prc, prs, xq)
         h = ts(T.bits[:, b:384:3], zs[b][:, 0:128], 0.0, float(2 ** b), OP.is_lt, OP.mult, z)
     bs = scan(T.bs[:], T.rstb[:], T.bits[:], h, c_rb)
-    bucket = T.bs[:, 2:384:3]
-
-    def match(half):
-        for i in range(4 * half, 4 * half + 4):
-            h = ts(T.mt[:, 128 * i:128 * i + 128], bucket, float(pos[i]), None, OP.is_equal, None, bs)
-        return scan(T.cu[:, 512 * half:512 * half + 512], T.rst1[:], T.mt[:, 512 * half:512 * half + 512], h, c_r1)
-
-    def sums_s(half, cu):
-        for i in range(4 * half, 4 * half + 4):
-            w = slice(128 * i, 128 * i + 128)
-            h = do("s", lambda: S.activation(T.junk1[:, w], T.cu[:, w], SIGN, T.bi[:, 1:2], -1.0, accum_out=T.acc1[:, i:i + 1]), cu, c_bi)
-        return h
-
-    def sums_v(half, cu):
-        w = slice(512 * half, 512 * half + 512)
-        h = ts(T.cm[:, w], T.cu[:, w], T.rh[:, 0:1], None, OP.is_le, None, cu)
-        return scan(T.su[:, w], T.rst1[:], T.cm[:, w], h)
-
-    def offsets(half, sv, ss):
-        vcopy(T.off1[:, 8 * half:8 * half + 8:2], T.su[:, 512 * half + 127:512 * half + 512:128], sv)
-        return ts(T.off1[:, 8 * half + 1:8 * half + 8:2], T.acc1[:, 4 * half:4 * half + 4], 0.5, 64.0, OP.mult, OP.add, ss)
 
     XQ, L1, CC = ("xq", "xs"), ("land1c", "land1s"), ("ccc", "ccs")
-    cu0 = match(0)
-    ss0 = sums_s(0, cu0)
-    sv0 = sums_v(0, cu0)
-    cu1 = match(1)
-    o0 = offsets(0, sv0, ss0)
+    for e in range(2):
+        h = ts(T.mt[:, 128 * e:128 * e + 128], T.bs[:, 2:384:3], T.dq[:, e:e + 1], None, OP.is_equal, None, bs, i_dq)
+    cu = scan(T.cu[:], T.rst1[:], T.mt[:], h, c_r1)
+    for e in range(2):
+        w = slice(128 * e, 128 * e + 128)
+        hs = count_s(T.acc1[:, e:e + 1], T.junk1[:, w], T.cu[:, w], T.bi[:, 1:2], cu, c_bi)
+    h = ts(T.cm[:], T.cu[:], T.rh[:, 0:1], None, OP.is_le, None, cu)
+    h = scan(T.su[:], T.rst1[:], T.cm[:], h)
+    ts(T.lq[:, 4:6], T.cu[:, 127:256:128], 4096.0, T.wq2[:, 0:1], OP.mult, OP.min, i_wq)
+    vcopy(T.lq[:, 0:4:2], T.su[:, 127:256:128], h)
+    lq = ts(T.lq[:, 1:4:2], T.acc1[:], 0.5, 64.0, OP.mult, OP.add, hs)
+    la = quads(lambda b, a: quad("la", b, slice(6 * a, 6 * a + 6)), lambda a: quad("lq", a, slice(0, 6)), lq)
+
+    def offsets(e):
+        vcopy(T.off1[:, 8 * e:8 * e + 8:2], T.la[:, 2 * e:24:6], *la)
+        return vcopy(T.off1[:, 8 * e + 1:8 * e + 8:2], T.la[:, 2 * e + 1:24:6])
+
+    o0 = offsets(0)
     pc, ps = pick("slot1", XQ, 130, 0, 128, T.off1[:, 0:8], o0, xq)
-    send_cross("slot1c", "r1c", "rc1", pc)
-    send_cross("slot1s", "r1s", "rs1", ps)
-    ss1 = sums_s(1, cu1)
-    sv1 = sums_v(1, cu1)
-    c_mk = ts(T.mk[:], T.q8[:], p16, None, OP.is_equal, None, i_q8)
-    for i in range(N):
-        c_wf = vset(T.wf[:, i:i + 1], 256.0 * 2 ** (i % 4))
-    h = ts(T.fl1[:], T.cu[:, 127:1024:128], 4096.0, None, OP.mult, None, cu0, cu1)
-    tt(T.rr[:, 8:16], T.fl1[:], T.wf[:], OP.min, h, c_wf)
-    o1 = offsets(1, sv1, ss1)
-    h = vcopy(T.offf[:], T.off1[:], o1, o0)
-    tt(T.rr[:, 0:8], T.offf[:, 0:8], T.mk[:, 0:8], OP.mult, h, c_mk)
-    h = tt(T.rr[:, 16:24], T.offf[:, 8:16], T.mk[:, 8:16], OP.mult, h)
-    red(T.mf[:, 0:1], T.rr[:, 0:12], OP.add, h)
-    h = red(T.mf[:, 1:2], T.rr[:, 12:24], OP.add, h)
-    m1 = vcopy(T.m1[:], T.mf[:], h)
-    q, q8 = by8(me), by8(me, 8)
-    own_n = vcopy(T.nl1[:, q8:q8 + 1], T.mf[:, 1:2], h)
-    send_note(T.m1[:, 1:2], T.m1[:, 0:1], "nl1", q8, T.rm[:, 0:1], "n1", "rn1", m1)
+    send_cross(1, "slot1c", "r1c", "rc1", pc)
+    send_cross(1, "slot1s", "r1s", "rs1", ps)
+    o1 = offsets(1)
+    h = ts(T.rr[:, 0:2], T.mk[:], p16, None, OP.is_equal, None, i_hb)
+    for e in range(2):
+        vcopy(T.rr[:, 4 + 4 * e:8 + 4 * e], T.la[:, 4 + e:24:6])
+        h = tt(T.lq[:, 2 * e:2 * e + 2], T.lq[:, 2 * e:2 * e + 2], T.rr[:, 0:2], OP.mult, h, *la)
+    for e in range(2):
+        red(T.mf[:, e:e + 1], T.lq[:, 2 * e:2 * e + 2], OP.add, h)
+        h2 = red(T.mf[:, 2 + e:3 + e], T.rr[:, 4 + 4 * e:8 + 4 * e], OP.add, h)
+    h = tt(T.mf[:, 4:6], T.mf[:, 0:2], T.mf[:, 2:4], OP.add, h2)
+    m1 = vcopy(T.m1[:], T.mf[:, 4:6], h)
+    own_n = vcopy(T.nl1[:, 8 * me:8 * me + 1], T.mf[:, 5:6], h)
+    send_note(T.m1[:, 1:2], T.m1[:, 0:1], "nl1", T.rm[:, 0:1], "n1", "rn1", m1)
     pc, ps = pick("slot1", XQ, 130, 128, 256, T.off1[:, 8:16], o1, xq)
-    send_same("slot1c", "land1c", q, "a1", pc)
-    send_same("slot1s", "land1s", q, "a1", ps)
+    send_same("slot1c", "land1c", "a1", pc)
+    send_same("slot1s", "land1s", "a1", ps)
     i = pos.index(me)
-    own1 = pick("land1", XQ, 130, q, q + 32, T.off1[:, 2 * i:2 * i + 2], o1, xq)
+    own1 = pick("land1", XQ, 130, 32 * me, 32 * me + 32, T.off1[:, 2 * i:2 * i + 2], o1, xq)
 
     load("y", "ldz", T.land3c[:, 256:258].bitcast(dt.uint8), T.xq[:, 128:130].bitcast(dt.uint8), xq)
     ldz = load("y", "ldz", T.land3s[:, 256:258], T.xs[:, 128:130], xq)
     h = vset(T.dm0[:], 0.9375)
-    c_dm = do("p", lambda: g.affine_select(T.dm[:], T.dm0[:], [[-1, 128]], OP.is_equal, 0.0, 0, 1), h)
-    h = ts(T.cp[:, 0:1], p32, 32.0, pf, OP.mult, OP.add, c_pb)
-    c_cp = ts(T.cp[:, 1:2], T.cp[:, 0:1], 32.0, None, OP.add, None, h)
-    for b in range(2):
-        c_tri = ts(T.tri[:, 256 * b:256 * b + 256], T.cc0[:], T.cp[:, b:b + 1], -BIG, OP.is_ge, OP.mult, c_cp, i_cc)
-    c_tt = vset(T.tt[:], 0.0)
+    c_dm = do("p", lambda: g.affine_select(T.dm[:], T.dm0[:], [[-1, 128]], OP.is_equal, 0.0, 0, 1), h, i_cc)
+    c_cp = ts(T.cp1[:], pf, 128.0, None, OP.add, None)
+    ts(T.tri[:, 0:128], T.cc0[:, 0:128], pf, -BIG, OP.is_ge, OP.mult, i_cc)
+    c_tri = ts(T.tri[:, 128:384], T.cc0[:], T.cp1[:, 0:1], -BIG, OP.is_ge, OP.mult, c_cp)
+    c_one = vset(T.one[:], 1.0)
     vset(T.nb[:], 0.0)
     h = vset(T.rst2[:], 1.0)
-    c_r2 = vset(T.rst2[:, 0:NV * 256:256], 0.0, h)
+    c_r2 = vset(T.rst2[:, 0:512:256], 0.0, h)
     h = vset(T.rst9[:], 1.0)
     vset(T.rst9[:, 0:72:9], 0.0, h)
-    c_one = vset(T.one8[:], 1.0)
+    h = ts(T.k8[:, 0:1], p32, 64.0, rho, OP.mult, OP.add)
+    h = ts(T.rq[:], T.rhc[:], T.k8[:, 0:1], None, OP.add, None, h)
+    c_bq = ts(T.bq[:], T.rq[:], 0.5, None, OP.add, None, h)
     ts(T.ma[:], T.q4[:], p32, None, OP.is_equal, None, i_q4)
-    h = ts(T.k8[:, 0:1], rho, 8.0, None, OP.mult, None)
+    h = ts(T.k8[:, 0:1], rho, 8.0, None, OP.mult, None, c_bq)
     ts(T.k8[:, 1:2], T.k8[:, 0:1], 128.0, None, OP.add, None, h)
     c_gg = ts(T.gg[:], T.ggc[:], T.k8[:, 0:1], None, OP.add, None, h, i_gg)
     vcopy(T.it[:, 0:72:9], T.gg[:], c_gg)
@@ -316,74 +325,72 @@ def rank_program(g, core, T, topo):
     h = ts(T.ff[:], T.fi[:], -256.0, None, OP.mult, None, h)
     h = tt(T.ft[:], T.ff[:], T.c32[:], OP.add, h, i_c32)
     h = red(T.k0[:], T.ft[:], OP.min, h)
-    ts(T.eg[:, 0:2], T.cp[:], T.k0[:, 0:1], None, OP.is_equal, None, h, c_cp)
-    eq = ts(T.eg[:, 2:4], T.cp[:], T.k0[:, 0:1], None, OP.is_ge, None, h)
+    for b, c in enumerate((pf, T.cp1[:, 0:1])):
+        ts(T.eg[:, b:b + 1], c, T.k0[:, 0:1], None, OP.is_equal, None, h)
+        eq = ts(T.eg[:, 2 + b:3 + b], c, T.k0[:, 0:1], None, OP.is_ge, None)
     gs, gm, th = [T.ga, T.gb], [], []
     for b in range(2):
         w = slice(128 * b, 128 * b + 128)
-        gm.append(do("t", lambda: E.matmul_mx(gs[b][:, 0:256], T.land1c[:, w], T.land1s[:, w], T.land1c[:], T.land1s[:], True, True), a1, *own1))
+        n = 128 + 128 * b
+        gm.append(do("t", lambda: E.matmul_mx(gs[b][:, 0:n], T.land1c[:, w], T.land1s[:, w], T.land1c[:, 0:n], T.land1s[:, 0:n], True, True), a1, *own1))
     for b in range(2):
         w = slice(128 * b, 128 * b + 128)
         h = tt(T.pd[:, w], gs[b][:, w], T.dm[:], OP.mult, gm[b], c_dm)
         th.append(do("s", lambda: S.activation(T.junk2[:, w], T.pd[:, w], COPY, accum_out=T.thr[:, b:b + 1]), h))
     for b in range(2):
-        w = slice(256 * b, 256 * b + 256)
-        h = tt(T.xg[:, w], gs[b][:, 0:256], T.tri[:, w], OP.add, c_tri)
+        n = 128 + 128 * b
+        w = slice(128 * b, 128 * b + n)
+        h = tt(T.xg[:, w], gs[b][:, 0:n], T.tri[:, w], OP.add, c_tri)
         h = red(T.mx[:, b:b + 1], T.xg[:, w], OP.max, h)
     h = tt(T.f12[:, 0:2], T.mx[:], T.thr[:], OP.is_lt, h, th[1])
     h = tt(T.f12[:, 2:4], T.f12[:, 0:2], T.eg[:, 0:2], OP.max, h)
-    h = tt(T.tt[:, 0:64:32], T.f12[:, 2:4], T.eg[:, 2:4], OP.mult, h, eq, c_tt)
-    tr = turn(T.tr[:], T.tt[:], h)
-    for a in range(4):
-        bc = do("p", lambda: g.partition_broadcast(T.bc[:, 64 * a:64 * a + 64], T.tr[32 * a:32 * a + 1, :], 128), tr)
+    for b in range(2):
+        h2 = ts(T.tt[:, 32 * b:32 * b + 32], T.one[:], T.f12[:, 2 + b:3 + b], T.eg[:, 2 + b:3 + b], OP.mult, OP.mult, h, eq, c_one)
+    for b in range(2):
+        tr = turn(T.tw[:, b, :], T.tt[:, 32 * b:32 * b + 32], h2)
+    bc = quads(lambda b, a: quad("bc", b, slice(0, 2), slice(32 * a, 32 * a + 32)), lambda a: quad("tw", a, slice(0, 2), slice(0, 32)), tr)
+    h = scan(T.cum[:, 0:128], T.rst2[:, 1:129], T.bc[:, 0, :], *bc)
+    cum = scan(T.cum[:, 128:256], T.rst2[:, 1:129], T.bc[:, 1, :], h, c_r2, init=T.cum[:, 127:128])
+
+    send_note(T.cum[:, 255:256], T.cum[:, 255:256], "cl", T.rm2[:, 0:1], "c2", "rn2", cum)
+    for c in range(2):
+        w = slice(256 * c, 256 * c + 256)
+        sa = count_s(T.acc2[:, c:c + 1], T.junk3[:, w], T.cum[:], T.bq[:, 2 + c:3 + c], cum, c_bq)
+        h = ts(T.cm2[:, w], T.cum[:], T.rq[:, c:c + 1], None, OP.is_le, None, cum)
+    h = scan(T.su2[:], T.rst2[:], T.cm2[:], h)
+    vcopy(T.nq[:, 0:2], T.su2[:, 255:512:256], h)
+    h = ts(T.nq[:, 2:4], T.acc2[:], 0.5, 128.0, OP.mult, OP.add, sa)
+    na = quads(lambda b, a: quad("na", b, slice(4 * a, 4 * a + 4)), lambda a: quad("nq", a, slice(0, 4)), h)
+    oc = ts(T.offc[:], T.na[:], 255.0, None, OP.min, None, *na)
+    ck = pick("cc", L1, 256, 0, 256, T.offc[:], oc, a1, *own1)
+    own_c = vcopy(T.cl[:, 8 * me:8 * me + 1], T.cum[:, 255:256])
     h = ts(T.jn[:], T.ni[:], 255, None, OP.bitwise_and, None)
     h = tt(T.nb[:, 0:256:32], T.jn[:], T.c128[:], OP.add, h, i_c128)
     nt = turn(T.nt[:], T.nb[:], h)
-    cum = scan(T.cum[:], T.rst2[:, 0:256], T.bc[:], bc, c_r2)
-
-    send_note(T.cum[:, 255:256], T.cum[:, 255:256], "cl", 8 * me, T.rm2[:, 0:1], "c2", "rn2", cum)
     nw = do("p", lambda: g.partition_broadcast(T.nw[:], T.nt[32 * am:32 * am + 1, :], 128), nt)
-    own_c = vcopy(T.cl[:, 8 * me:8 * me + 1], T.cum[:, 255:256], cum)
-    for c in range(NS):
-        w = slice(256 * c, 256 * c + 256)
-        sa = do("s", lambda: S.activation(T.junk3[:, w], T.cum[:], SIGN, T.bi[:, NV + c:NV + c + 1], -1.0, accum_out=T.acc2[:, c:c + 1]), cum)
-    for c in range(NV):
-        h = ts(T.cm2[:, 256 * c:256 * c + 256], T.cum[:], T.rh[:, c:c + 1], None, OP.is_le, None)
-    h = scan(T.su2[:], T.rst2[:], T.cm2[:], h)
-    vcopy(T.nn[:, 0:NV], T.su2[:, 255:NV * 256:256], h)
-    h = ts(T.nn[:, NV:16], T.acc2[:], 0.5, 128.0, OP.mult, OP.add, sa)
-    t = [T.at[:, 16 * i:16 * i + 16] for i in range(6)]
-    ts(t[0], T.nn[:], 31, None, OP.bitwise_and, None, h)
-    ts(t[1], T.nn[:], 1, 96, OP.logical_shift_right, OP.bitwise_and)
-    h = ts(t[2], T.nn[:], 32, None, OP.bitwise_and, None)
-    tt(t[3], t[0], t[1], OP.add, h)
-    h = ts(t[4], t[2], 4.0, None, OP.mult, None, h)
-    h = tt(t[5], t[3], t[4], OP.add, h)
-    oc = vcopy(T.offc[:], t[5], h)
-    ck = pick("cc", L1, 256, 0, 256, T.offc[:], oc, a1, *own1)
     nwc = act(T.nwc[:], T.nw[:].indirect(T.offc[:]), oc, nw)
 
-    end = scan(T.end[:], T.one8[:], T.cl[:, 0:64:8], ("c2", nmsg), own_c, c_one)
+    end = scan(T.end[:], T.one[:, 0:8], T.cl[:, 0:64:8], ("c2", nmsg), own_c)
     h = ts(T.vi[:], T.rc[:], T.end[:, me - 1:me] if me else 0.0, None, OP.subtract, None, end)
     h = ts(T.v7[:], T.vi[:], 7, None, OP.bitwise_and, None, h)
     ts(T.off3[:, 0:16:2], T.v7[:], T.k8[:, 0:1], None, OP.add, None, h)
     o3 = ts(T.off3[:, 1:16:2], T.v7[:], T.k8[:, 1:2], None, OP.add, None)
     pc, ps = pick("slot3", CC, 256, 0, 128, T.off3[:, 0:8], o3, *ck)
-    send_cross("slot3c", "r3c", "rc3", pc)
-    send_cross("slot3s", "r3s", "rs3", ps)
-    pc, ps = pick("slot3", CC, 256, 128, 256, T.off3[:, 8:16], o3, *ck)
-    send_same("slot3c", "land3c", 32 * me, "a3", pc)
-    send_same("slot3s", "land3s", 32 * me, "a3", ps)
+    send_cross(3, "slot3c", "r3c", "rc3", pc)
+    send_cross(3, "slot3s", "r3s", "rs3", ps)
     n3 = act(T.n3[:], T.nwc[:].indirect(T.off3[:]), o3, nwc)
-    i = pos.index(me)
-    own3 = pick("land3", CC, 256, 32 * me, 32 * me + 32, T.off3[:, 2 * i:2 * i + 2], o3, *ck)
+    pc, ps = pick("slot3", CC, 256, 128, 256, T.off3[:, 8:16], o3, *ck)
     h = turn(T.nt3[:], T.n3[:], n3)
     h = tt(T.nm[:], T.nt3[:, 0:256:32], T.ma[:], OP.mult, h)
     red(T.m3f[:, 0:1], T.nm[:, 0:4], OP.add, h)
     h = red(T.m3f[:, 1:2], T.nm[:, 4:8], OP.add, h)
     m3 = vcopy(T.m3[:], T.m3f[:], h)
+    send_note(T.m3[:, 1:2], T.m3[:, 0:1], "nl3", T.rm[:, 8:9], "n3", "rn3", m3)
+    send_same("slot3c", "land3c", "a3", pc)
+    send_same("slot3s", "land3s", "a3", ps)
     own_n3 = vcopy(T.nl3[:, 8 * me:8 * me + 1], T.m3f[:, 1:2], h)
-    send_note(T.m3[:, 1:2], T.m3[:, 0:1], "nl3", 8 * me, T.rm[:, 8:9], "n3", "rn3", m3)
+    i = pos.index(me)
+    own3 = pick("land3", CC, 256, 32 * me, 32 * me + 32, T.off3[:, 2 * i:2 * i + 2], o3, *ck)
 
     h = ts(T.d256[:], T.cl[:, 0:64:8], -1.0, 256.0, OP.mult, OP.add)
     for d in range(N):

@@ -3,6 +3,7 @@ from concourse.mybir import dt, AluOpType, AxisListType, ActivationFunctionType
 
 OP = AluOpType
 COPY = ActivationFunctionType.Copy
+IDENT = ActivationFunctionType.Identity
 SIGN = ActivationFunctionType.Sign
 X = AxisListType.X
 N, P, L, CAPP = 8, 128, 3, 32
@@ -11,13 +12,13 @@ BIG = 1.0e29
 SCRATCH = {}
 for _kind, _list in {
     "bfloat16": "plh 512 xh 520 wh 512 rstb 384 rst1 256 rst2 512 one 32 bits 384 bs 384 mt 256 cu 256 cm 256 su 256 junk1 256 "
-                "tt 64 cum 256 cm2 512 su2 512 junk3 512 cl 64 rm2 1",
+                "tt 64 cum 256 cm2 512 su2 512 junk3 512 cl 64 rm2 1 m1 2 nl1 64 rm1 1",
     "float8_e4m3fn_x4": "plc 128 prc 384 xq 130 wq 128 slot1c 256 land1c 256 ccc 256 slot3c 256 land3c 258 fq 128 r1c 64 r3c 64",
     "uint8": "pls 128 prs 384 xs 130 ws 128 slot1s 256 land1s 256 ccs 256 slot3s 256 land3s 258 fs 128 r1s 64 r3s 64",
-    "uint16": "ofp 24 off1 16 m1 2 nl1 64 offc 16 off3 16 nl3 64 m3 2 offz 8 rm 24",
-    "int32": "pb 4 ni 8 fi 8 jn 8 vi 8 v7 8 xi 8 xsh 8",
-    "float32": "rst9 72 pbf 4 q4 8 cc0 256 c32 8 c128 8 rhc 4 rh 4 bi 4 rq 4 bq 4 ggc 8 gg 8 k8 2 dm0 128 dm 128 mk 2 ma 8 cp1 1 tri 384 "
-               "rc 8 dq 2 wq2 1 acc1 2 lq 6 la 24 rr 12 mf 6 ff 8 ft 8 k0 1 eg 4 pd 256 junk2 256 thr 2 xg 384 mx 2 f12 4 nb 256 nt 256 "
+    "uint16": "ofp 24 off1 16 offc 16 off3 16 nl3 64 m3 2 offz 8 rm3 1",
+    "int32": "pb 4 vi 8 v7 8 xi 8 xsh 8",
+    "float32": "rst9 72 pbf 4 nx 1 q4 8 cc0 256 c127 8 c128 8 rhc 4 rh 4 bi 4 rq 4 bq 4 ggc 8 gg 8 k8 2 dm0 128 dm 128 ma 8 cp 2 cps 2 tri 384 "
+               "rc 8 dq 2 acc1 2 la1 2 em 8 ep 8 k0 1 ab 8 pd 256 junk2 256 thr 2 thb 2 xg 384 mx 2 nb 256 nt 256 "
                "nw 256 acc2 2 nq 4 na 16 nwc 256 end 8 n3 256 nt3 256 nm 8 m3f 2 d256 8 it 72 its 72 nf 256 nft 264 no 128 ysb 128",
 }.items():
     _w = _list.split()
@@ -27,6 +28,8 @@ for _n in ("z0", "z1", "z2", "ga", "gb", "yp"):
     SCRATCH[_n] = ("psum", [128, 512], "float32")
 SCRATCH["tw"] = ("sbuf", [128, 2, 32], "bfloat16")
 SCRATCH["bc"] = ("sbuf", [128, 2, 128], "bfloat16")
+SCRATCH["lq"] = ("sbuf", [128, 2, 2], "float32")
+SCRATCH["la"] = ("sbuf", [128, 2, 8], "float32")
 SEMAPHORES = ["qv", "qs", "qt", "qp", "ldp", "ldx", "ldw", "ldz", "dout", "ls",
               "a1", "n1", "c2", "a3", "n3", "rc1", "rs1", "rn1", "rn2", "rc3", "rs3", "rn3"]
 
@@ -49,9 +52,10 @@ def dest(topo, src, dst):
     return DstId(rid=rid, pnc=pid)
 
 
-COL_PEER, COL_FAR, COL_RELAY = 8, 4, 4
-MSG_PEER, MSG_FAR, MSG_RELAY = 4, 8, 8
-HAND = {1: ((8, 12), (12, 16)), 3: ((0, 8), (8, 16))}
+HAND = ((0, 8), (8, 16))
+COL = {"peer": (8, 16), 0: (0, 4), 1: (4, 8)}
+MSG = {"far": (0, 4), "peer": (4, 8)}
+SIZE = {"far": (0, 8), "peer": (8, 16)}
 
 
 def view(T, buf, a, b):
@@ -63,28 +67,27 @@ def relay_program(g, core, T, topo, s, group):
     to = [T.cores[r] for r in group]
     sent = [0]
 
-    def go(sem, n, tr):
-        g.wait_ge(T.sem[sem], n)
+    def go(sem, tr):
+        g.wait_ge(T.sem[sem], 8)
         g.remote_dma_fused(tr, local_sem=T.sem.ls)
         sent[0] += 8
 
-    def cols(sem, n, buf, land, rsem):
+    def cols(sem, buf, land, rsem):
         at = 32 * s
-        go(sem, n, [RemoteDMATransfer(dst_ids=[dest(topo, core, d)], dma_engine_mask=eng(topo, core, d, 4 * i, 4 * i + 4), remote_sem=T.sem[rsem],
-                                      src=view(T, buf, 32 * i, 32 * i + 32), dst=view(T, land, at, at + 32)) for i, d in enumerate(to)])
+        go(sem, [RemoteDMATransfer(dst_ids=[dest(topo, core, d)], dma_engine_mask=eng(topo, core, d, 4 * i, 4 * i + 4), remote_sem=T.sem[rsem],
+                                   src=view(T, buf, 32 * i, 32 * i + 32), dst=view(T, land, at, at + 32)) for i, d in enumerate(to)])
 
     def note(sem, src, land, rsem):
-        go(sem, 4, [RemoteDMATransfer(dst_ids=[dest(topo, core, d) for d in to], dma_engine_mask=eng(topo, core, to[0], 0, 8), remote_sem=T.sem[rsem],
-                                      srcs=[src], dsts=[T[land][:, 8 * s:8 * s + 1]] * 2)])
+        go(sem, [RemoteDMATransfer(dst_ids=[dest(topo, core, d) for d in to], dma_engine_mask=eng(topo, core, to[0], 0, 8), remote_sem=T.sem[rsem],
+                                   srcs=[T[src][:]], dsts=[T[land][:, 8 * s:8 * s + 1]] * 2)])
 
-    n1, n3 = [HAND[k][0][1] - HAND[k][0][0] for k in (1, 3)]
-    cols("rc1", n1, "r1c", "land1c", "a1")
-    cols("rs1", n1, "r1s", "land1s", "a1")
-    note("rn1", T.rm[:, 0:1], "nl1", "n1")
-    note("rn2", T.rm2[:, 0:1], "cl", "c2")
-    cols("rc3", n3, "r3c", "land3c", "a3")
-    cols("rs3", n3, "r3s", "land3s", "a3")
-    note("rn3", T.rm[:, 8:9], "nl3", "n3")
+    note("rn1", "rm1", "nl1", "n1")
+    cols("rc1", "r1c", "land1c", "a1")
+    cols("rs1", "r1s", "land1s", "a1")
+    note("rn2", "rm2", "cl", "c2")
+    cols("rc3", "r3c", "land3c", "a3")
+    cols("rs3", "r3s", "land3s", "a3")
+    note("rn3", "rm3", "nl3", "n3")
     g.wait_ge(T.sem.ls, sent[0])
 
 
@@ -102,8 +105,9 @@ def rank_program(g, core, T, topo):
     am = same.index(me)
     peer = [r for r in same if r != me and T.cores[r] in topo.cores_of(core)]
     far = [r for r in same if r != me and r not in peer]
-    ncol = sum(COL_PEER if r in peer else COL_FAR if r in far else COL_RELAY for r in range(N) if r != me)
-    nmsg = sum(MSG_PEER if r in peer else MSG_FAR if r in far else MSG_RELAY for r in range(N) if r != me)
+    ncol = 8 * len(peer) + 4 * len(far) + 4 * len(cross)
+    nmsg = 4 * len(peer) + 4 * len(far) + 8 * len(cross)
+    nsize = 8 * len(peer) + 8 * len(far) + 8 * len(cross)
 
     V, S, E, Y = g.vector, g.scalar, g.tensor, g.sync
     Q = {"v": V, "s": S, "t": E, "p": g, "y": Y}
@@ -148,14 +152,17 @@ def rank_program(g, core, T, topo):
     def red(out, in_, op, *deps):
         return do("v", lambda: V.tensor_reduce(out, in_, X, op), *deps)
 
-    def scan(out, d0, d1, *deps, init=0.0):
-        return do("v", lambda: V.tensor_tensor_scan(out, d0, d1, init, OP.mult, OP.add), *deps)
+    def scan(out, d0, d1, *deps, init=0.0, op1=OP.add):
+        return do("v", lambda: V.tensor_tensor_scan(out, d0, d1, init, OP.mult, op1), *deps)
 
     def turn(out, in_, *deps):
         return do("v", lambda: V.transpose(out, in_), *deps)
 
     def act(out, in_, *deps):
         return do("s", lambda: S.activation(out, in_, COPY), *deps)
+
+    def affine(out, in_, scale, bias, *deps):
+        return do("s", lambda: S.activation(out, in_, IDENT, bias, scale), *deps)
 
     def count_s(out, junk, in_, bias, *deps):
         return do("s", lambda: S.activation(junk, in_, SIGN, bias, -1.0, accum_out=out), *deps)
@@ -166,13 +173,13 @@ def rank_program(g, core, T, topo):
             return do("p", lambda: g.iota(ap, pattern, base, cm, allow_small_or_imprecise_dtypes=True), last)
         return do("p", lambda: g.iota(ap, pattern, base, cm), last)
 
-    def quads(out, in_, *deps):
-        for a in range(4):
-            for b in range(4):
-                if b % 2:
-                    hs = act(out(b, a), in_(a), *deps)
-                else:
-                    hv = vcopy(out(b, a), in_(a), *deps)
+    def quads(ns, out, in_, *deps):
+        for k in range(16):
+            a, b = k // 4, k % 4
+            if k * ns % 16 < ns:
+                hs = act(out(b, a), in_(a), *deps)
+            else:
+                hv = vcopy(out(b, a), in_(a), *deps)
         return hv, hs
 
     def quad(t, a, *cols):
@@ -189,25 +196,26 @@ def rank_program(g, core, T, topo):
         g.remote_dma_fused([t for t, n in tr], local_sem=T.sem.ls)
         cnt["ls"] = cnt.get("ls", 0) + sum(n for t, n in tr)
 
-    def xfer(src, dst, to, a, b, sem):
-        return (RemoteDMATransfer(dst_ids=[dest(topo, core, c) for c in to], dma_engine_mask=eng(topo, core, to[0], a, b), remote_sem=T.sem[sem],
-                                  srcs=[src], dsts=[dst] * len(to)), b - a)
+    def xfer(src, dst, to, ab, sem):
+        return (RemoteDMATransfer(dst_ids=[dest(topo, core, c) for c in to], dma_engine_mask=eng(topo, core, to[0], ab[0], ab[1]),
+                                  remote_sem=T.sem[sem], srcs=[src], dsts=[dst] * len(to)), ab[1] - ab[0])
 
-    def send_cross(stage, buf, rbuf, sem, *deps):
-        send([xfer(view(T, buf, 64 * i, 64 * i + 64), view(T, rbuf, 0, 64), [k], HAND[stage][i][0], HAND[stage][i][1], sem)
-              for i, k in enumerate(relays)], *deps)
+    def send_cross(buf, rbuf, sem, *deps):
+        send([xfer(view(T, buf, 64 * i, 64 * i + 64), view(T, rbuf, 0, 64), [k], HAND[i], sem) for i, k in enumerate(relays)], *deps)
 
     def send_same(buf, land, sem, *deps):
         tr, at = [], 32 * me
         for i, r in enumerate(far + peer):
-            a, e = 32 * pos.index(r), (8, 16) if r in peer else (4 * i, 4 * i + 4)
-            tr.append(xfer(view(T, buf, a, a + 32), view(T, land, at, at + 32), [T.cores[r]], e[0], e[1], sem))
+            a = 32 * pos.index(r)
+            tr.append(xfer(view(T, buf, a, a + 32), view(T, land, at, at + 32), [T.cores[r]], COL["peer" if r in peer else i], sem))
         send(tr, *deps)
 
-    def send_note(to_same, to_cross, land, rbuf, sem, rsem, *deps):
+    def own_parity(src, land, e, sem):
         dst = T[land][:, 8 * me:8 * me + 1]
-        send([xfer(to_same, dst, [T.cores[r] for r in far], 0, 8, sem), xfer(to_cross, rbuf, relays, 8, 12, rsem),
-              xfer(to_same, dst, [T.cores[r] for r in peer], 12, 16, sem)], *deps)
+        return [xfer(src, dst, [T.cores[r] for r in far], e["far"], sem), xfer(src, dst, [T.cores[r] for r in peer], e["peer"], sem)]
+
+    def send_note(src, land, rbuf, sem, rsem, *deps):
+        send([xfer(src[:, 0:1], T[rbuf][:], relays, (8, 16), rsem)] + own_parity(src[:, 1:2], land, MSG, sem), *deps)
 
     ldp = load("y", "ldp", T.plh[:, 0:16], T.pl[:, 0:16])
     ldx = load("s", "ldx", T.xh[:, 0:512], T.x[:])
@@ -217,13 +225,11 @@ def rank_program(g, core, T, topo):
     for a in range(4):
         for e in range(2):
             i_dq = iota(quad("dq", a, slice(e, e + 1)), [[0, 1]], pos[4 * e + a])
-    for a in range(4):
-        i_wq = iota(quad("wq2", a, slice(0, 1)), [[0, 1]], 256 * 2 ** a)
-    i_hb = iota(T.mk[:], [[1, 2]], 0)
-    i_q4 = iota(T.q4[:], [[0, 2], [1, 4]], 0)
-    i_c32 = iota(T.c32[:], [[32, 8]], 256)
-    i_c128 = iota(T.c128[:], [[128, 8]], 0)
-    i_gg = iota(T.ggc[:], [[128, 8]], me)
+    iota(T.q4[:], [[0, 2], [1, 4]], 0)
+    iota(T.c128[:], [[128, 8]], 0)
+    iota(T.c127[:], [[128, 8]], P - 1)
+    iota(T.ggc[:], [[128, 8]], me)
+    i_cp = iota(T.cp[:], [[128, 2]], 0, 1)
     i_cc = iota(T.cc0[:], [[1, 256]], 0)
     c_pl = vset(T.plh[:, 16:512], 0.0)
     c_x = vset(T.xh[:, 512:520], 0.0)
@@ -237,8 +243,9 @@ def rank_program(g, core, T, topo):
     ts(T.pb[:, 2:3], T.pb[:, 0:1], 4, 1, OP.logical_shift_right, OP.bitwise_and)
     h = ts(T.pb[:, 3:4], T.pb[:, 0:1], 5, None, OP.logical_shift_right, None)
     c_pb = vcopy(T.pbf[:], T.pb[:], h)
-    pf, rho, p16, p32 = [T.pbf[:, i:i + 1] for i in range(4)]
+    rho, p16, p32 = [T.pbf[:, i:i + 1] for i in (1, 2, 3)]
     c_rh = ts(T.rh[:], T.rhc[:], rho, None, OP.add, None, c_pb, i_rh)
+    ts(T.nx[:], p16, -1.0, 1.0, OP.mult, OP.add)
     c_bi = ts(T.bi[:], T.rh[:], 0.5, None, OP.add, None, c_rh)
 
     h = do("v", lambda: V.quantize_mx(T.plc[:], T.pls[:], T.plh[:]), ldp, c_pl)
@@ -261,46 +268,35 @@ def rank_program(g, core, T, topo):
         hs = count_s(T.acc1[:, e:e + 1], T.junk1[:, w], T.cu[:, w], T.bi[:, 1:2], cu, c_bi)
     h = ts(T.cm[:], T.cu[:], T.rh[:, 0:1], None, OP.is_le, None, cu)
     h = scan(T.su[:], T.rst1[:], T.cm[:], h)
-    ts(T.lq[:, 4:6], T.cu[:, 127:256:128], 4096.0, T.wq2[:, 0:1], OP.mult, OP.min, i_wq)
-    vcopy(T.lq[:, 0:4:2], T.su[:, 127:256:128], h)
-    lq = ts(T.lq[:, 1:4:2], T.acc1[:], 0.5, 64.0, OP.mult, OP.add, hs)
-    la = quads(lambda b, a: quad("la", b, slice(6 * a, 6 * a + 6)), lambda a: quad("lq", a, slice(0, 6)), lq)
-
-    def offsets(e):
-        vcopy(T.off1[:, 8 * e:8 * e + 8:2], T.la[:, 2 * e:24:6], *la)
-        return vcopy(T.off1[:, 8 * e + 1:8 * e + 8:2], T.la[:, 2 * e + 1:24:6])
-
-    o0 = offsets(0)
+    vcopy(T.lq[:, :, 0], T.su[:, 127:256:128], h)
+    ts(T.la1[:], T.su[:, 127:256:128], T.nx[:, 0:1], None, OP.mult, None)
+    lq = ts(T.lq[:, :, 1], T.acc1[:], 0.5, 64.0, OP.mult, OP.add, hs)
+    for e in range(2):
+        m1 = affine(T.m1[:, e:e + 1], T.lq[:, e, 1:2], p16, T.la1[:, e:e + 1], lq)
+    send_note(T.m1, "nl1", "rm1", "n1", "rn1", m1)
+    la = quads(6, lambda b, a: quad("la", b, slice(0, 2), slice(2 * a, 2 * a + 2)), lambda a: quad("lq", a, slice(0, 2), slice(0, 2)), lq)
+    o0 = vcopy(T.off1[:, 0:8], T.la[:, 0, :], *la)
     pc, ps = pick("slot1", XQ, 130, 0, 128, T.off1[:, 0:8], o0, xq)
-    send_cross(1, "slot1c", "r1c", "rc1", pc)
-    send_cross(1, "slot1s", "r1s", "rs1", ps)
-    o1 = offsets(1)
-    h = ts(T.rr[:, 0:2], T.mk[:], p16, None, OP.is_equal, None, i_hb)
-    for e in range(2):
-        vcopy(T.rr[:, 4 + 4 * e:8 + 4 * e], T.la[:, 4 + e:24:6])
-        h = tt(T.lq[:, 2 * e:2 * e + 2], T.lq[:, 2 * e:2 * e + 2], T.rr[:, 0:2], OP.mult, h, *la)
-    for e in range(2):
-        red(T.mf[:, e:e + 1], T.lq[:, 2 * e:2 * e + 2], OP.add, h)
-        h2 = red(T.mf[:, 2 + e:3 + e], T.rr[:, 4 + 4 * e:8 + 4 * e], OP.add, h)
-    h = tt(T.mf[:, 4:6], T.mf[:, 0:2], T.mf[:, 2:4], OP.add, h2)
-    m1 = vcopy(T.m1[:], T.mf[:, 4:6], h)
-    own_n = vcopy(T.nl1[:, 8 * me:8 * me + 1], T.mf[:, 5:6], h)
-    send_note(T.m1[:, 1:2], T.m1[:, 0:1], "nl1", T.rm[:, 0:1], "n1", "rn1", m1)
+    send_cross("slot1c", "r1c", "rc1", pc)
+    send_cross("slot1s", "r1s", "rs1", ps)
+    o1 = vcopy(T.off1[:, 8:16], T.la[:, 1, :])
     pc, ps = pick("slot1", XQ, 130, 128, 256, T.off1[:, 8:16], o1, xq)
     send_same("slot1c", "land1c", "a1", pc)
     send_same("slot1s", "land1s", "a1", ps)
     i = pos.index(me)
     own1 = pick("land1", XQ, 130, 32 * me, 32 * me + 32, T.off1[:, 2 * i:2 * i + 2], o1, xq)
+    own_n = vcopy(T.nl1[:, 8 * me:8 * me + 1], T.m1[:, 1:2], m1)
 
     load("y", "ldz", T.land3c[:, 256:258].bitcast(dt.uint8), T.xq[:, 128:130].bitcast(dt.uint8), xq)
     ldz = load("y", "ldz", T.land3s[:, 256:258], T.xs[:, 128:130], xq)
+    c_nb = vset(T.nb[:], 0.0)
     h = vset(T.dm0[:], 0.9375)
     c_dm = do("p", lambda: g.affine_select(T.dm[:], T.dm0[:], [[-1, 128]], OP.is_equal, 0.0, 0, 1), h, i_cc)
-    c_cp = ts(T.cp1[:], pf, 128.0, None, OP.add, None)
-    ts(T.tri[:, 0:128], T.cc0[:, 0:128], pf, -BIG, OP.is_ge, OP.mult, i_cc)
-    c_tri = ts(T.tri[:, 128:384], T.cc0[:], T.cp1[:, 0:1], -BIG, OP.is_ge, OP.mult, c_cp)
+    ts(T.cps[:], T.cp[:], 1.0 / 32, None, OP.mult, None, i_cp)
+    for b in range(2):
+        w = 128 + 128 * b
+        c_tri = ts(T.tri[:, 128 * b:128 * b + w], T.cc0[:, 0:w], T.cp[:, b:b + 1], -BIG, OP.is_ge, OP.mult, i_cc)
     c_one = vset(T.one[:], 1.0)
-    vset(T.nb[:], 0.0)
     h = vset(T.rst2[:], 1.0)
     c_r2 = vset(T.rst2[:, 0:512:256], 0.0, h)
     h = vset(T.rst9[:], 1.0)
@@ -308,10 +304,10 @@ def rank_program(g, core, T, topo):
     h = ts(T.k8[:, 0:1], p32, 64.0, rho, OP.mult, OP.add)
     h = ts(T.rq[:], T.rhc[:], T.k8[:, 0:1], None, OP.add, None, h)
     c_bq = ts(T.bq[:], T.rq[:], 0.5, None, OP.add, None, h)
-    ts(T.ma[:], T.q4[:], p32, None, OP.is_equal, None, i_q4)
+    ts(T.ma[:], T.q4[:], p32, None, OP.is_equal, None)
     h = ts(T.k8[:, 0:1], rho, 8.0, None, OP.mult, None, c_bq)
     ts(T.k8[:, 1:2], T.k8[:, 0:1], 128.0, None, OP.add, None, h)
-    c_gg = ts(T.gg[:], T.ggc[:], T.k8[:, 0:1], None, OP.add, None, h, i_gg)
+    c_gg = ts(T.gg[:], T.ggc[:], T.k8[:, 0:1], None, OP.add, None, h)
     vcopy(T.it[:, 0:72:9], T.gg[:], c_gg)
     for i in range(N):
         vset(T.rc[:, i:i + 1], 2048.0 + pos[i])
@@ -320,39 +316,45 @@ def rank_program(g, core, T, topo):
     c_all = do("v", lambda: V.quantize_mx(T.wq[:], T.ws[:], T.wh[:]), ldw)
 
     a1, n1 = ("a1", 2 * ncol), ("n1", nmsg)
-    ni = vcopy(T.ni[:], T.nl1[:, 0:64:8], n1, own_n)
-    h = ts(T.fi[:], T.ni[:], 8 + am, 1, OP.logical_shift_right, OP.bitwise_and, ni)
-    h = ts(T.ff[:], T.fi[:], -256.0, None, OP.mult, None, h)
-    h = tt(T.ft[:], T.ff[:], T.c32[:], OP.add, h, i_c32)
-    h = red(T.k0[:], T.ft[:], OP.min, h)
-    for b, c in enumerate((pf, T.cp1[:, 0:1])):
-        ts(T.eg[:, b:b + 1], c, T.k0[:, 0:1], None, OP.is_equal, None, h)
-        eq = ts(T.eg[:, 2 + b:3 + b], c, T.k0[:, 0:1], None, OP.is_ge, None)
-    gs, gm, th = [T.ga, T.gb], [], []
+    h = tt(T.nb[:, 0:256:32], T.nl1[:, 0:64:8], T.c128[:], OP.add, n1, own_n, c_nb, i_cc)
+    nt = turn(T.nt[:], T.nb[:], h)
+    nw = do("p", lambda: g.partition_broadcast(T.nw[:], T.nt[32 * am:32 * am + 1, :], 128), nt, c_dm)
+    h = tt(T.em[:], T.nw[:, 0:256:32], T.c127[:], OP.is_gt, nw)
+    h = scan(T.ep[:], T.em[:], T.one[:, 0:8], h, c_one, init=1.0, op1=OP.mult)
+    h = red(T.k0[:], T.ep[:], OP.add, h)
+    k0 = T.k0[:, 0:1]
+    ts(T.ab[:, 0:2], T.cps[:], k0, None, OP.is_gt, None, h)
+    ts(T.ab[:, 4:6], T.cps[:], k0, 2 * BIG, OP.is_equal, OP.mult)
+    h = ts(T.ab[:, 6:8], T.cps[:], k0, -2 * BIG, OP.is_lt, OP.mult)
+    ab = tt(T.ab[:, 2:4], T.ab[:, 4:6], T.ab[:, 6:8], OP.add, h)
+
+    gs, gm = [T.ga, T.gb], []
+    wd = [(slice(128 * b, 128 * b + 128), slice(128 * b, 128 + 256 * b), 128 + 128 * b) for b in range(2)]
     for b in range(2):
-        w = slice(128 * b, 128 * b + 128)
-        n = 128 + 128 * b
+        w, w2, n = wd[b]
         gm.append(do("t", lambda: E.matmul_mx(gs[b][:, 0:n], T.land1c[:, w], T.land1s[:, w], T.land1c[:, 0:n], T.land1s[:, 0:n], True, True), a1, *own1))
     for b in range(2):
-        w = slice(128 * b, 128 * b + 128)
+        w, w2, n = wd[b]
         h = tt(T.pd[:, w], gs[b][:, w], T.dm[:], OP.mult, gm[b], c_dm)
-        th.append(do("s", lambda: S.activation(T.junk2[:, w], T.pd[:, w], COPY, accum_out=T.thr[:, b:b + 1]), h))
+        h = do("s", lambda: S.activation(T.junk2[:, w], T.pd[:, w], COPY, accum_out=T.thr[:, b:b + 1]), h)
+        th = affine(T.thb[:, b:b + 1], T.thr[:, b:b + 1], T.ab[:, b:b + 1], T.ab[:, 2 + b:3 + b], h, ab)
+    hx, hr, hl, tr = [], [], [], []
     for b in range(2):
-        n = 128 + 128 * b
-        w = slice(128 * b, 128 * b + n)
-        h = tt(T.xg[:, w], gs[b][:, 0:n], T.tri[:, w], OP.add, c_tri)
-        h = red(T.mx[:, b:b + 1], T.xg[:, w], OP.max, h)
-    h = tt(T.f12[:, 0:2], T.mx[:], T.thr[:], OP.is_lt, h, th[1])
-    h = tt(T.f12[:, 2:4], T.f12[:, 0:2], T.eg[:, 0:2], OP.max, h)
+        w, w2, n = wd[b]
+        hx.append(tt(T.xg[:, w2], gs[b][:, 0:n], T.tri[:, w2], OP.add, c_tri))
     for b in range(2):
-        h2 = ts(T.tt[:, 32 * b:32 * b + 32], T.one[:], T.f12[:, 2 + b:3 + b], T.eg[:, 2 + b:3 + b], OP.mult, OP.mult, h, eq, c_one)
+        hr.append(red(T.mx[:, b:b + 1], T.xg[:, wd[b][1]], OP.max, hx[b]))
     for b in range(2):
-        tr = turn(T.tw[:, b, :], T.tt[:, 32 * b:32 * b + 32], h2)
-    bc = quads(lambda b, a: quad("bc", b, slice(0, 2), slice(32 * a, 32 * a + 32)), lambda a: quad("tw", a, slice(0, 2), slice(0, 32)), tr)
+        hl.append(ts(T.tt[:, 32 * b:32 * b + 32], T.one[:], T.mx[:, b:b + 1], T.thb[:, b:b + 1], OP.mult, OP.is_lt, hr[b], th))
+    for b in range(2):
+        tr.append(turn(T.tw[:, b, :], T.tt[:, 32 * b:32 * b + 32], hl[b]))
+    bc = quads(7, lambda b, a: quad("bc", b, slice(0, 2), slice(32 * a, 32 * a + 32)), lambda a: quad("tw", a, slice(0, 2), slice(0, 32)), *tr)
     h = scan(T.cum[:, 0:128], T.rst2[:, 1:129], T.bc[:, 0, :], *bc)
     cum = scan(T.cum[:, 128:256], T.rst2[:, 1:129], T.bc[:, 1, :], h, c_r2, init=T.cum[:, 127:128])
 
-    send_note(T.cum[:, 255:256], T.cum[:, 255:256], "cl", T.rm2[:, 0:1], "c2", "rn2", cum)
+    size = T.cum[:, 255:256]
+    send([xfer(size, T.rm2[:], [k], HAND[i], "rn2") for i, k in enumerate(relays)], cum)
+    send(own_parity(size, "cl", SIZE, "c2"))
     for c in range(2):
         w = slice(256 * c, 256 * c + 256)
         sa = count_s(T.acc2[:, c:c + 1], T.junk3[:, w], T.cum[:], T.bq[:, 2 + c:3 + c], cum, c_bq)
@@ -360,24 +362,20 @@ def rank_program(g, core, T, topo):
     h = scan(T.su2[:], T.rst2[:], T.cm2[:], h)
     vcopy(T.nq[:, 0:2], T.su2[:, 255:512:256], h)
     h = ts(T.nq[:, 2:4], T.acc2[:], 0.5, 128.0, OP.mult, OP.add, sa)
-    na = quads(lambda b, a: quad("na", b, slice(4 * a, 4 * a + 4)), lambda a: quad("nq", a, slice(0, 4)), h)
+    na = quads(7, lambda b, a: quad("na", b, slice(4 * a, 4 * a + 4)), lambda a: quad("nq", a, slice(0, 4)), h)
     oc = ts(T.offc[:], T.na[:], 255.0, None, OP.min, None, *na)
     ck = pick("cc", L1, 256, 0, 256, T.offc[:], oc, a1, *own1)
-    own_c = vcopy(T.cl[:, 8 * me:8 * me + 1], T.cum[:, 255:256])
-    h = ts(T.jn[:], T.ni[:], 255, None, OP.bitwise_and, None)
-    h = tt(T.nb[:, 0:256:32], T.jn[:], T.c128[:], OP.add, h, i_c128)
-    nt = turn(T.nt[:], T.nb[:], h)
-    nw = do("p", lambda: g.partition_broadcast(T.nw[:], T.nt[32 * am:32 * am + 1, :], 128), nt)
+    own_c = vcopy(T.cl[:, 8 * me:8 * me + 1], size)
     nwc = act(T.nwc[:], T.nw[:].indirect(T.offc[:]), oc, nw)
 
-    end = scan(T.end[:], T.one[:, 0:8], T.cl[:, 0:64:8], ("c2", nmsg), own_c)
+    end = scan(T.end[:], T.one[:, 0:8], T.cl[:, 0:64:8], ("c2", nsize), own_c)
     h = ts(T.vi[:], T.rc[:], T.end[:, me - 1:me] if me else 0.0, None, OP.subtract, None, end)
     h = ts(T.v7[:], T.vi[:], 7, None, OP.bitwise_and, None, h)
     ts(T.off3[:, 0:16:2], T.v7[:], T.k8[:, 0:1], None, OP.add, None, h)
     o3 = ts(T.off3[:, 1:16:2], T.v7[:], T.k8[:, 1:2], None, OP.add, None)
     pc, ps = pick("slot3", CC, 256, 0, 128, T.off3[:, 0:8], o3, *ck)
-    send_cross(3, "slot3c", "r3c", "rc3", pc)
-    send_cross(3, "slot3s", "r3s", "rs3", ps)
+    send_cross("slot3c", "r3c", "rc3", pc)
+    send_cross("slot3s", "r3s", "rs3", ps)
     n3 = act(T.n3[:], T.nwc[:].indirect(T.off3[:]), o3, nwc)
     pc, ps = pick("slot3", CC, 256, 128, 256, T.off3[:, 8:16], o3, *ck)
     h = turn(T.nt3[:], T.n3[:], n3)
@@ -385,7 +383,7 @@ def rank_program(g, core, T, topo):
     red(T.m3f[:, 0:1], T.nm[:, 0:4], OP.add, h)
     h = red(T.m3f[:, 1:2], T.nm[:, 4:8], OP.add, h)
     m3 = vcopy(T.m3[:], T.m3f[:], h)
-    send_note(T.m3[:, 1:2], T.m3[:, 0:1], "nl3", T.rm[:, 8:9], "n3", "rn3", m3)
+    send_note(T.m3, "nl3", "rm3", "n3", "rn3", m3)
     send_same("slot3c", "land3c", "a3", pc)
     send_same("slot3s", "land3s", "a3", ps)
     own_n3 = vcopy(T.nl3[:, 8 * me:8 * me + 1], T.m3f[:, 1:2], h)

@@ -11,15 +11,15 @@ BIG = 1.0e29
 
 SCRATCH = {}
 for _kind, _list in {
-    "bfloat16": "plh 512 xh 520 wh 512 rstb 384 rst1 256 rst2 512 one 32 bits 384 bs 384 mt 256 cu 256 cm 256 su 256 junk1 256 "
-                "tt 64 cum 256 cm2 512 su2 512 junk3 512 cl 64 rm2 1 m1 2 nl1 64 rm1 1",
+    "bfloat16": "plh 512 xh 520 wh 512 rstb 384 rst2 512 one 32 bits 384 bs 384 mt 256 cu 256 cm 256 junk1 256 "
+                "tt 64 cum 256 cm2 512 su2 512 junk3 512 cl 64 rm2 1 m1 2 nl1 64 rm1 1 n8 8",
     "float8_e4m3fn_x4": "plc 128 prc 384 xq 130 wq 128 slot1c 256 land1c 256 ccc 256 slot3c 256 land3c 258 fq 128 r1c 64 r3c 64",
     "uint8": "pls 128 prs 384 xs 130 ws 128 slot1s 256 land1s 256 ccs 256 slot3s 256 land3s 258 fs 128 r1s 64 r3s 64",
-    "uint16": "ofp 24 off1 16 offc 16 off3 16 nl3 64 m3 2 offz 8 rm3 1",
-    "int32": "pb 4 vi 8 v7 8 xi 8 xsh 8",
-    "float32": "rst9 72 pbf 4 nx 1 q4 8 cc0 256 c127 8 c128 8 rhc 4 rh 4 bi 4 rq 4 bq 4 ggc 8 gg 8 k8 2 dm0 128 dm 128 ma 8 cp 2 cps 2 tri 384 "
-               "rc 8 dq 2 acc1 2 la1 2 em 8 ep 8 k0 1 ab 8 pd 256 junk2 256 thr 2 thb 2 xg 384 mx 2 nb 256 nt 256 "
-               "nw 256 acc2 2 nq 4 na 16 nwc 256 end 8 n3 256 nt3 256 nm 8 m3f 2 d256 8 it 72 its 72 nf 256 nft 264 no 128 ysb 128",
+    "uint16": "ofp 24 off1 16 offc 16 off3 20 nl3 64 m3 2 offz 8 rm3 1",
+    "int32": "pb 4 vi 10 v7 10 xi 8 xsh 8",
+    "float32": "rst9 72 pbf 4 nx 1 off 24 c32 64 ccr 256 c128 8 rhc 4 rh 4 bi 4 rq 4 bq 4 ggc 8 gg 8 k8 2 dm0 128 dm 128 cp 2 tri 384 "
+               "rc 10 dq 2 acc1 2 la1 2 em 8 ep 8 k0 1 ab 64 ab1 64 ab2 64 pd 256 junk2 256 thr 2 xg 384 nb 256 nt 256 "
+               "nw 256 acc2 2 nq 4 na 16 nwc 256 end 8 n3 64 nt3 64 d256 8 it 72 its 72 nf 256 nft 264 no 128 ysb 128",
 }.items():
     _w = _list.split()
     for _i in range(0, len(_w), 2):
@@ -54,8 +54,7 @@ def dest(topo, src, dst):
 
 HAND = ((0, 8), (8, 16))
 COL = {"peer": (8, 16), 0: (0, 4), 1: (4, 8)}
-MSG = {"far": (0, 4), "peer": (4, 8)}
-SIZE = {"far": (0, 8), "peer": (8, 16)}
+MSG = {"relay": (8, 16), "far": (0, 8), "peer": (8, 16)}
 
 
 def view(T, buf, a, b):
@@ -106,8 +105,7 @@ def rank_program(g, core, T, topo):
     peer = [r for r in same if r != me and T.cores[r] in topo.cores_of(core)]
     far = [r for r in same if r != me and r not in peer]
     ncol = 8 * len(peer) + 4 * len(far) + 4 * len(cross)
-    nmsg = 4 * len(peer) + 4 * len(far) + 8 * len(cross)
-    nsize = 8 * len(peer) + 8 * len(far) + 8 * len(cross)
+    nmsg = 8 * (N - 1)
 
     V, S, E, Y = g.vector, g.scalar, g.tensor, g.sync
     Q = {"v": V, "s": S, "t": E, "p": g, "y": Y}
@@ -155,6 +153,9 @@ def rank_program(g, core, T, topo):
     def scan(out, d0, d1, *deps, init=0.0, op1=OP.add):
         return do("v", lambda: V.tensor_tensor_scan(out, d0, d1, init, OP.mult, op1), *deps)
 
+    def runs(out, in_, *deps):
+        return do("v", lambda: V.tensor_tensor_scan(out, in_, in_, 0.0, OP.add, OP.max), *deps)
+
     def turn(out, in_, *deps):
         return do("v", lambda: V.transpose(out, in_), *deps)
 
@@ -173,14 +174,14 @@ def rank_program(g, core, T, topo):
             return do("p", lambda: g.iota(ap, pattern, base, cm, allow_small_or_imprecise_dtypes=True), last)
         return do("p", lambda: g.iota(ap, pattern, base, cm), last)
 
-    def quads(ns, out, in_, *deps):
-        for k in range(16):
-            a, b = k // 4, k % 4
-            if k * ns % 16 < ns:
+    def spread(ns, out, in_, half, *deps):
+        for k in range(8):
+            a, b = k // 2, k // 2 ^ k % 2
+            if k * ns % 8 < ns:
                 hs = act(out(b, a), in_(a), *deps)
             else:
                 hv = vcopy(out(b, a), in_(a), *deps)
-        return hv, hs
+        return vcopy(half(1, 0), half(0, 0), hv, hs), act(half(0, 1), half(1, 1), hv, hs)
 
     def quad(t, a, *cols):
         return T[t][(slice(32 * a, 32 * a + 32),) + cols]
@@ -210,76 +211,78 @@ def rank_program(g, core, T, topo):
             tr.append(xfer(view(T, buf, a, a + 32), view(T, land, at, at + 32), [T.cores[r]], COL["peer" if r in peer else i], sem))
         send(tr, *deps)
 
-    def own_parity(src, land, e, sem):
-        dst = T[land][:, 8 * me:8 * me + 1]
-        return [xfer(src, dst, [T.cores[r] for r in far], e["far"], sem), xfer(src, dst, [T.cores[r] for r in peer], e["peer"], sem)]
+    def note(src, land, sem, to, ab):
+        return xfer(src, T[land][:, 8 * me:8 * me + 1], [T.cores[r] for r in to], ab, sem)
 
-    def send_note(src, land, rbuf, sem, rsem, *deps):
-        send([xfer(src[:, 0:1], T[rbuf][:], relays, (8, 16), rsem)] + own_parity(src[:, 1:2], land, MSG, sem), *deps)
+    def note_out(src, rbuf, rsem, *deps):
+        send([xfer(src[:, 0:1], T[rbuf][:], relays, MSG["relay"], rsem)], *deps)
+
+    def note_same(src, land, sem, *deps):
+        send([note(src, land, sem, far, MSG["far"]), note(src, land, sem, peer, MSG["peer"])], *deps)
 
     ldp = load("y", "ldp", T.plh[:, 0:16], T.pl[:, 0:16])
     ldx = load("s", "ldx", T.xh[:, 0:512], T.x[:])
     ldw = load("y", "ldw", T.wh[:], T.w[:], ldx)
+    i_of = iota(T.off[:], [[1, L], [0, 8]], 0)
     i_p = iota(T.pb[:, 0:1], [[1, 1]], 0, 1, False)
     i_rh = iota(T.rhc[:], [[16, 4]], 0)
     for a in range(4):
-        for e in range(2):
-            i_dq = iota(quad("dq", a, slice(e, e + 1)), [[0, 1]], pos[4 * e + a])
-    iota(T.q4[:], [[0, 2], [1, 4]], 0)
+        i_dq = iota(quad("dq", a, slice(0, 2)), [[pos[4 + a] - pos[a], 2]], pos[a])
     iota(T.c128[:], [[128, 8]], 0)
-    iota(T.c127[:], [[128, 8]], P - 1)
     iota(T.ggc[:], [[128, 8]], me)
-    i_cp = iota(T.cp[:], [[128, 2]], 0, 1)
-    i_cc = iota(T.cc0[:], [[1, 256]], 0)
+    iota(T.cp[:], [[128, 2]], 0, 1)
+    iota(T.c32[:], [[128, 2], [0, 32]], 0, 1)
+    i_cc = iota(T.ccr[:], [[-1, 256]], 255)
     c_pl = vset(T.plh[:, 16:512], 0.0)
-    c_x = vset(T.xh[:, 512:520], 0.0)
-    for b in range(L):
-        c_of = vset(T.ofp[:, 8 * b:8 * b + 8], b)
     h = vset(T.rstb[:], 1.0)
-    c_rb = vset(T.rstb[:, 0:384:3], 0.0, h)
-    h = vset(T.rst1[:], 1.0)
-    c_r1 = vset(T.rst1[:, 0:256:128], 0.0, h)
+    c_of = vcopy(T.ofp[:], T.off[:], i_of)
+    c_x = vset(T.xh[:, 512:520], 0.0)
     ts(T.pb[:, 1:2], T.pb[:, 0:1], 15, None, OP.bitwise_and, None, i_p)
     ts(T.pb[:, 2:3], T.pb[:, 0:1], 4, 1, OP.logical_shift_right, OP.bitwise_and)
-    h = ts(T.pb[:, 3:4], T.pb[:, 0:1], 5, None, OP.logical_shift_right, None)
-    c_pb = vcopy(T.pbf[:], T.pb[:], h)
+    h2 = ts(T.pb[:, 3:4], T.pb[:, 0:1], 5, None, OP.logical_shift_right, None)
+    c_rb = vset(T.rstb[:, 0:384:3], 0.0, h)
+    c_pb = vcopy(T.pbf[:], T.pb[:], h2)
     rho, p16, p32 = [T.pbf[:, i:i + 1] for i in (1, 2, 3)]
-    c_rh = ts(T.rh[:], T.rhc[:], rho, None, OP.add, None, c_pb, i_rh)
-    ts(T.nx[:], p16, -1.0, 1.0, OP.mult, OP.add)
-    c_bi = ts(T.bi[:], T.rh[:], 0.5, None, OP.add, None, c_rh)
+    c_rh = affine(T.rh[:], T.rhc[:], 1.0, rho, c_pb, i_rh)
 
-    h = do("v", lambda: V.quantize_mx(T.plc[:], T.pls[:], T.plh[:]), ldp, c_pl)
-    prc = pickc(T.prc[:], T.plc[:], T.ofp[:], h, c_of)
-    prs = act(T.prs[:], T.pls[:].indirect(T.ofp[:]), h, c_of)
-    xq = do("v", lambda: V.quantize_mx(T.xq[:], T.xs[:], T.xh[:]), ldx, c_x)
+    plq = do("v", lambda: V.quantize_mx(T.plc[:], T.pls[:], T.plh[:]), ldp, c_pl)
+    pr = []
+    for b in range(L):
+        w, o = slice(128 * b, 128 * b + 128), slice(8 * b, 8 * b + 8)
+        hv = pickc(T.prc[:, w], T.plc[:], T.ofp[:, o], plq, c_of)
+        pr.append((hv, act(T.prs[:, w], T.pls[:].indirect(T.ofp[:, o]), plq, c_of)))
+        if b == 0:
+            xq = do("v", lambda: V.quantize_mx(T.xq[:], T.xs[:], T.xh[:]), ldx, c_x)
+    ts(T.nx[:], p16, -1.0, 1.0, OP.mult, OP.add, c_pb)
+    c_bi = ts(T.bi[:], T.rhc[:], rho, 0.5, OP.add, OP.add, i_rh)
     zs = [T.z0, T.z1, T.z2]
     for b in range(L):
         w = slice(128 * b, 128 * b + 128)
-        z = do("t", lambda: E.matmul_mx(zs[b][:, 0:128], T.prc[:, w], T.prs[:, w], T.xq[:, 0:128], T.xs[:, 0:128], True, True), prc, prs, xq)
+        z = do("t", lambda: E.matmul_mx(zs[b][:, 0:128], T.prc[:, w], T.prs[:, w], T.xq[:, 0:128], T.xs[:, 0:128], True, True), xq, *pr[b])
         h = ts(T.bits[:, b:384:3], zs[b][:, 0:128], 0.0, float(2 ** b), OP.is_lt, OP.mult, z)
     bs = scan(T.bs[:], T.rstb[:], T.bits[:], h, c_rb)
 
     XQ, L1, CC = ("xq", "xs"), ("land1c", "land1s"), ("ccc", "ccs")
+    w2 = [slice(128 * e, 128 * e + 128) for e in range(2)]
+    hm = [ts(T.mt[:, w], T.bs[:, 2:384:3], T.dq[:, e:e + 1], None, OP.is_equal, None, bs, i_dq) for e, w in enumerate(w2)]
+    cu = [runs(T.cu[:, w], T.mt[:, w], hm[e]) for e, w in enumerate(w2)]
+    hs = [count_s(T.acc1[:, e:e + 1], T.junk1[:, w], T.cu[:, w], T.bi[:, 1:2], cu[e], c_bi) for e, w in enumerate(w2)]
+    hc = [ts(T.cm[:, w], T.cu[:, w], T.rh[:, 0:1], None, OP.is_le, None, cu[e], c_rh) for e, w in enumerate(w2)]
+    h0 = [red(T.lq[:, e, 0:1], T.cm[:, w], OP.add, hc[e]) for e, w in enumerate(w2)]
+    hl = ts(T.la1[:], T.lq[:, :, 0], T.nx[:, 0:1], None, OP.mult, None, *h0)
     for e in range(2):
-        h = ts(T.mt[:, 128 * e:128 * e + 128], T.bs[:, 2:384:3], T.dq[:, e:e + 1], None, OP.is_equal, None, bs, i_dq)
-    cu = scan(T.cu[:], T.rst1[:], T.mt[:], h, c_r1)
-    for e in range(2):
-        w = slice(128 * e, 128 * e + 128)
-        hs = count_s(T.acc1[:, e:e + 1], T.junk1[:, w], T.cu[:, w], T.bi[:, 1:2], cu, c_bi)
-    h = ts(T.cm[:], T.cu[:], T.rh[:, 0:1], None, OP.is_le, None, cu)
-    h = scan(T.su[:], T.rst1[:], T.cm[:], h)
-    vcopy(T.lq[:, :, 0], T.su[:, 127:256:128], h)
-    ts(T.la1[:], T.su[:, 127:256:128], T.nx[:, 0:1], None, OP.mult, None)
-    lq = ts(T.lq[:, :, 1], T.acc1[:], 0.5, 64.0, OP.mult, OP.add, hs)
-    for e in range(2):
-        m1 = affine(T.m1[:, e:e + 1], T.lq[:, e, 1:2], p16, T.la1[:, e:e + 1], lq)
-    send_note(T.m1, "nl1", "rm1", "n1", "rn1", m1)
-    la = quads(6, lambda b, a: quad("la", b, slice(0, 2), slice(2 * a, 2 * a + 2)), lambda a: quad("lq", a, slice(0, 2), slice(0, 2)), lq)
+        lq = ts(T.lq[:, e, 1:2], T.acc1[:, e:e + 1], 0.5, 64.0, OP.mult, OP.add, hs[e])
+        m1 = affine(T.m1[:, e:e + 1], T.lq[:, e, 1:2], p16, T.la1[:, e:e + 1], lq, hl)
+        if e == 0:
+            note_out(T.m1, "rm1", "rn1", m1)
+    la = spread(3, lambda b, a: quad("la", b, slice(0, 2), slice(2 * a, 2 * a + 2)), lambda a: quad("lq", a, slice(0, 2), slice(0, 2)),
+                lambda b, a: T.la[64 * b:64 * b + 64, :, 4 * a:4 * a + 4], lq, *h0)
     o0 = vcopy(T.off1[:, 0:8], T.la[:, 0, :], *la)
+    o1 = vcopy(T.off1[:, 8:16], T.la[:, 1, :])
     pc, ps = pick("slot1", XQ, 130, 0, 128, T.off1[:, 0:8], o0, xq)
     send_cross("slot1c", "r1c", "rc1", pc)
     send_cross("slot1s", "r1s", "rs1", ps)
-    o1 = vcopy(T.off1[:, 8:16], T.la[:, 1, :])
+    note_same(T.m1[:, 1:2], "nl1", "n1", m1)
     pc, ps = pick("slot1", XQ, 130, 128, 256, T.off1[:, 8:16], o1, xq)
     send_same("slot1c", "land1c", "a1", pc)
     send_same("slot1s", "land1s", "a1", ps)
@@ -292,10 +295,9 @@ def rank_program(g, core, T, topo):
     c_nb = vset(T.nb[:], 0.0)
     h = vset(T.dm0[:], 0.9375)
     c_dm = do("p", lambda: g.affine_select(T.dm[:], T.dm0[:], [[-1, 128]], OP.is_equal, 0.0, 0, 1), h, i_cc)
-    ts(T.cps[:], T.cp[:], 1.0 / 32, None, OP.mult, None, i_cp)
     for b in range(2):
         w = 128 + 128 * b
-        c_tri = ts(T.tri[:, 128 * b:128 * b + w], T.cc0[:, 0:w], T.cp[:, b:b + 1], -BIG, OP.is_ge, OP.mult, i_cc)
+        c_tri = ts(T.tri[:, 128 * b:128 * b + w], T.ccr[:, 256 - w:256], T.cp[:, b:b + 1], BIG, OP.is_lt, OP.mult, i_cc)
     c_one = vset(T.one[:], 1.0)
     h = vset(T.rst2[:], 1.0)
     c_r2 = vset(T.rst2[:, 0:512:256], 0.0, h)
@@ -304,13 +306,13 @@ def rank_program(g, core, T, topo):
     h = ts(T.k8[:, 0:1], p32, 64.0, rho, OP.mult, OP.add)
     h = ts(T.rq[:], T.rhc[:], T.k8[:, 0:1], None, OP.add, None, h)
     c_bq = ts(T.bq[:], T.rq[:], 0.5, None, OP.add, None, h)
-    ts(T.ma[:], T.q4[:], p32, None, OP.is_equal, None)
     h = ts(T.k8[:, 0:1], rho, 8.0, None, OP.mult, None, c_bq)
     ts(T.k8[:, 1:2], T.k8[:, 0:1], 128.0, None, OP.add, None, h)
     c_gg = ts(T.gg[:], T.ggc[:], T.k8[:, 0:1], None, OP.add, None, h)
     vcopy(T.it[:, 0:72:9], T.gg[:], c_gg)
     for i in range(N):
         vset(T.rc[:, i:i + 1], 2048.0 + pos[i])
+    ts(T.rc[:, 8:10], T.dq[:], 2048.0, None, OP.add, None)
     vset(T.nf[:], 0.0)
     vset(T.nft[:, 256:264], -1.0)
     c_all = do("v", lambda: V.quantize_mx(T.wq[:], T.ws[:], T.wh[:]), ldw)
@@ -318,43 +320,40 @@ def rank_program(g, core, T, topo):
     a1, n1 = ("a1", 2 * ncol), ("n1", nmsg)
     h = tt(T.nb[:, 0:256:32], T.nl1[:, 0:64:8], T.c128[:], OP.add, n1, own_n, c_nb, i_cc)
     nt = turn(T.nt[:], T.nb[:], h)
-    nw = do("p", lambda: g.partition_broadcast(T.nw[:], T.nt[32 * am:32 * am + 1, :], 128), nt, c_dm)
-    h = tt(T.em[:], T.nw[:, 0:256:32], T.c127[:], OP.is_gt, nw)
-    h = scan(T.ep[:], T.em[:], T.one[:, 0:8], h, c_one, init=1.0, op1=OP.mult)
+    n8 = do("p", lambda: g.partition_broadcast(T.n8[:], T.nl1[32 * am:32 * am + 1, 0:64:8], 128), n1, own_n, c_dm)
+    nw = do("p", lambda: g.partition_broadcast(T.nw[:], T.nt[32 * am:32 * am + 1, :], 128), nt, n8)
+    h = ts(T.em[:], T.n8[:], P - 1.0, None, OP.is_gt, None, n8)
+    h = scan(T.ep[:], T.em[:], T.one[:, 0:8], h, c_one, init=32.0, op1=OP.mult)
     h = red(T.k0[:], T.ep[:], OP.add, h)
-    k0 = T.k0[:, 0:1]
-    ts(T.ab[:, 0:2], T.cps[:], k0, None, OP.is_gt, None, h)
-    ts(T.ab[:, 4:6], T.cps[:], k0, 2 * BIG, OP.is_equal, OP.mult)
-    h = ts(T.ab[:, 6:8], T.cps[:], k0, -2 * BIG, OP.is_lt, OP.mult)
-    ab = tt(T.ab[:, 2:4], T.ab[:, 4:6], T.ab[:, 6:8], OP.add, h)
+    ts(T.ab1[:], T.c32[:], T.k0[:, 0:1], -2 * BIG, OP.is_equal, OP.mult, h)
+    h = ts(T.ab2[:], T.c32[:], T.k0[:, 0:1], 2 * BIG, OP.is_lt, OP.mult)
+    ab = tt(T.ab[:], T.ab1[:], T.ab2[:], OP.add, h)
 
     gs, gm = [T.ga, T.gb], []
     wd = [(slice(128 * b, 128 * b + 128), slice(128 * b, 128 + 256 * b), 128 + 128 * b) for b in range(2)]
     for b in range(2):
         w, w2, n = wd[b]
         gm.append(do("t", lambda: E.matmul_mx(gs[b][:, 0:n], T.land1c[:, w], T.land1s[:, w], T.land1c[:, 0:n], T.land1s[:, 0:n], True, True), a1, *own1))
+    mx, th, hl, tr = [], [], [], []
     for b in range(2):
         w, w2, n = wd[b]
         h = tt(T.pd[:, w], gs[b][:, w], T.dm[:], OP.mult, gm[b], c_dm)
-        h = do("s", lambda: S.activation(T.junk2[:, w], T.pd[:, w], COPY, accum_out=T.thr[:, b:b + 1]), h)
-        th = affine(T.thb[:, b:b + 1], T.thr[:, b:b + 1], T.ab[:, b:b + 1], T.ab[:, 2 + b:3 + b], h, ab)
-    hx, hr, hl, tr = [], [], [], []
+        th.append(do("s", lambda: S.activation(T.junk2[:, w], T.pd[:, w], COPY, accum_out=T.thr[:, b:b + 1]), h))
+        mx.append(do("v", lambda: V.tensor_tensor_scan(T.xg[:, w2], gs[b][:, n - 1::-1], T.tri[:, w2], 0.0, OP.max, OP.min), c_tri))
     for b in range(2):
-        w, w2, n = wd[b]
-        hx.append(tt(T.xg[:, w2], gs[b][:, 0:n], T.tri[:, w2], OP.add, c_tri))
-    for b in range(2):
-        hr.append(red(T.mx[:, b:b + 1], T.xg[:, wd[b][1]], OP.max, hx[b]))
-    for b in range(2):
-        hl.append(ts(T.tt[:, 32 * b:32 * b + 32], T.one[:], T.mx[:, b:b + 1], T.thb[:, b:b + 1], OP.mult, OP.is_lt, hr[b], th))
+        w = slice(32 * b, 32 * b + 32)
+        at = 128 * b + wd[b][2] - 1
+        hl.append(ts(T.tt[:, w], T.ab[:, w], T.xg[:, at:at + 1], T.thr[:, b:b + 1], OP.add, OP.is_lt, mx[b], th[b], ab))
     for b in range(2):
         tr.append(turn(T.tw[:, b, :], T.tt[:, 32 * b:32 * b + 32], hl[b]))
-    bc = quads(7, lambda b, a: quad("bc", b, slice(0, 2), slice(32 * a, 32 * a + 32)), lambda a: quad("tw", a, slice(0, 2), slice(0, 32)), *tr)
+    bc = spread(4, lambda b, a: quad("bc", b, slice(0, 2), slice(32 * a, 32 * a + 32)), lambda a: quad("tw", a, slice(0, 2), slice(0, 32)),
+                lambda b, a: T.bc[64 * b:64 * b + 64, :, 64 * a:64 * a + 64], *tr)
     h = scan(T.cum[:, 0:128], T.rst2[:, 1:129], T.bc[:, 0, :], *bc)
     cum = scan(T.cum[:, 128:256], T.rst2[:, 1:129], T.bc[:, 1, :], h, c_r2, init=T.cum[:, 127:128])
 
     size = T.cum[:, 255:256]
     send([xfer(size, T.rm2[:], [k], HAND[i], "rn2") for i, k in enumerate(relays)], cum)
-    send(own_parity(size, "cl", SIZE, "c2"))
+    note_same(size, "cl", "c2")
     for c in range(2):
         w = slice(256 * c, 256 * c + 256)
         sa = count_s(T.acc2[:, c:c + 1], T.junk3[:, w], T.cum[:], T.bq[:, 2 + c:3 + c], cum, c_bq)
@@ -362,31 +361,30 @@ def rank_program(g, core, T, topo):
     h = scan(T.su2[:], T.rst2[:], T.cm2[:], h)
     vcopy(T.nq[:, 0:2], T.su2[:, 255:512:256], h)
     h = ts(T.nq[:, 2:4], T.acc2[:], 0.5, 128.0, OP.mult, OP.add, sa)
-    na = quads(7, lambda b, a: quad("na", b, slice(4 * a, 4 * a + 4)), lambda a: quad("nq", a, slice(0, 4)), h)
+    na = spread(4, lambda b, a: quad("na", b, slice(4 * a, 4 * a + 4)), lambda a: quad("nq", a, slice(0, 4)),
+                lambda b, a: T.na[64 * b:64 * b + 64, 8 * a:8 * a + 8], h)
     oc = ts(T.offc[:], T.na[:], 255.0, None, OP.min, None, *na)
     ck = pick("cc", L1, 256, 0, 256, T.offc[:], oc, a1, *own1)
     own_c = vcopy(T.cl[:, 8 * me:8 * me + 1], size)
     nwc = act(T.nwc[:], T.nw[:].indirect(T.offc[:]), oc, nw)
 
-    end = scan(T.end[:], T.one[:, 0:8], T.cl[:, 0:64:8], ("c2", nsize), own_c)
+    end = scan(T.end[:], T.one[:, 0:8], T.cl[:, 0:64:8], ("c2", nmsg), own_c)
     h = ts(T.vi[:], T.rc[:], T.end[:, me - 1:me] if me else 0.0, None, OP.subtract, None, end)
     h = ts(T.v7[:], T.vi[:], 7, None, OP.bitwise_and, None, h)
-    ts(T.off3[:, 0:16:2], T.v7[:], T.k8[:, 0:1], None, OP.add, None, h)
-    o3 = ts(T.off3[:, 1:16:2], T.v7[:], T.k8[:, 1:2], None, OP.add, None)
+    ts(T.off3[:, 0:20:2], T.v7[:], T.k8[:, 0:1], None, OP.add, None, h)
+    o3 = ts(T.off3[:, 1:20:2], T.v7[:], T.k8[:, 1:2], None, OP.add, None)
     pc, ps = pick("slot3", CC, 256, 0, 128, T.off3[:, 0:8], o3, *ck)
     send_cross("slot3c", "r3c", "rc3", pc)
     send_cross("slot3s", "r3s", "rs3", ps)
-    n3 = act(T.n3[:], T.nwc[:].indirect(T.off3[:]), o3, nwc)
+    n3 = act(T.n3[:], T.nwc[:].indirect(T.off3[:, 16:20]), o3, nwc)
     pc, ps = pick("slot3", CC, 256, 128, 256, T.off3[:, 8:16], o3, *ck)
     h = turn(T.nt3[:], T.n3[:], n3)
-    h = tt(T.nm[:], T.nt3[:, 0:256:32], T.ma[:], OP.mult, h)
-    red(T.m3f[:, 0:1], T.nm[:, 0:4], OP.add, h)
-    h = red(T.m3f[:, 1:2], T.nm[:, 4:8], OP.add, h)
-    m3 = vcopy(T.m3[:], T.m3f[:], h)
-    send_note(T.m3, "nl3", "rm3", "n3", "rn3", m3)
+    m3 = vcopy(T.m3[:], T.nt3[:, 0:64:32], h)
+    own_n3 = vcopy(T.nl3[:, 8 * me:8 * me + 1], T.nt3[:, 32:33])
+    note_out(T.m3, "rm3", "rn3", m3)
     send_same("slot3c", "land3c", "a3", pc)
     send_same("slot3s", "land3s", "a3", ps)
-    own_n3 = vcopy(T.nl3[:, 8 * me:8 * me + 1], T.m3f[:, 1:2], h)
+    note_same(T.m3[:, 1:2], "nl3", "n3", m3)
     i = pos.index(me)
     own3 = pick("land3", CC, 256, 32 * me, 32 * me + 32, T.off3[:, 2 * i:2 * i + 2], o3, *ck)
 

from concourse.bass import DstId, RemoteDMATransfer
from concourse.mybir import dt, AluOpType, AxisListType, ActivationFunctionType

OP = AluOpType
COPY = ActivationFunctionType.Copy
IDENT = ActivationFunctionType.Identity
SIGN = ActivationFunctionType.Sign
X = AxisListType.X
N, P, L, CAPP = 8, 128, 3, 32
BIG = 1.0e29

SCRATCH = {}
for _kind, _list in {
    "bfloat16": "plh 512 xh 520 wh 512 rstb 384 rst2 512 one 32 bits 384 bs 384 mt 256 cu 256 cm 256 junk1 256 "
                "tt 64 cum 256 cm2 512 su2 512 junk3 512 cl 64 rm2 1 m1 2 nl1 64 rm1 1 n8 8",
    "float8_e4m3fn_x4": "plc 128 prc 384 xq 130 wq 128 slot1c 256 land1c 256 ccc 256 slot3c 256 land3c 258 fq 128 r1c 64 r3c 64",
    "uint8": "pls 128 prs 384 xs 130 ws 128 slot1s 256 land1s 256 ccs 256 slot3s 256 land3s 258 fs 128 r1s 64 r3s 64",
    "uint16": "ofp 24 off1 16 offc 16 off3 20 nl3 64 m3 2 offz 8 rm3 1",
    "int32": "pb 4 vi 10 v7 10 xi 8 xsh 8",
    "float32": "rst9 72 pbf 4 nx 1 off 24 c32 64 ccr 256 c128 8 rhc 4 rh 4 bi 4 rq 4 bq 4 ggc 8 gg 8 k8 2 dm0 128 dm 128 cp 2 tri 384 "
               "rc 10 dq 2 acc1 2 la1 2 em 8 ep 8 k0 1 ab 64 ab1 64 ab2 64 pd 256 junk2 256 thr 2 xg 384 nb 256 nt 256 "
               "nw 256 acc2 2 nq 4 na 16 nwc 256 end 8 n3 64 nt3 64 d256 8 it 72 its 72 nf 256 nft 264 no 128 ysb 128",
}.items():
    _w = _list.split()
    for _i in range(0, len(_w), 2):
        SCRATCH[_w[_i]] = ("sbuf", [128, int(_w[_i + 1])], _kind)
for _n in ("z0", "z1", "z2", "ga", "gb", "yp"):
    SCRATCH[_n] = ("psum", [128, 512], "float32")
SCRATCH["tw"] = ("sbuf", [128, 2, 32], "bfloat16")
SCRATCH["bc"] = ("sbuf", [128, 2, 128], "bfloat16")
SCRATCH["lq"] = ("sbuf", [128, 2, 2], "float32")
SCRATCH["la"] = ("sbuf", [128, 2, 8], "float32")
SEMAPHORES = ["qv", "qs", "qt", "qp", "ldp", "ldx", "ldw", "ldz", "dout", "ls",
              "a1", "n1", "c2", "a3", "n3", "rc1", "rs1", "rn1", "rn2", "rc3", "rs3", "rn3"]


def wiring(T, topo):
    cores = T.cores
    same = [[r for r in range(N) if cores[r] in topo.cores_of(cores[s]) or topo.same_plane(cores[s], cores[r])] for s in range(N)]
    cross = [[r for r in range(N) if r not in same[s]] for s in range(N)]
    relays = [[k for k in topo.cores_of(c) if k not in cores and topo.die(k) == topo.die(c)
               and all(topo.may_write(k, cores[r]) for r in cross[s])][:2] for s, c in enumerate(cores)]
    return same, cross, relays


def eng(topo, src, dst, a, b):
    return sum(1 << e for e in topo.engines(src, dst)[a:b])


def dest(topo, src, dst):
    rid, pid = topo.addr(dst, src)
    return DstId(rid=rid, pnc=pid)


HAND = ((0, 8), (8, 16))
COL = {"peer": (8, 16), 0: (0, 4), 1: (4, 8)}
MSG = {"relay": (8, 16), "far": (0, 8), "peer": (8, 16)}


def view(T, buf, a, b):
    v = T[buf][:, a:b]
    return v.bitcast(dt.uint8) if buf[-1] == "c" else v


def relay_program(g, core, T, topo, s, group):
    to = [T.cores[r] for r in group]
    sent = [0]

    def go(sem, tr):
        g.wait_ge(T.sem[sem], 8)
        g.remote_dma_fused(tr, local_sem=T.sem.ls)
        sent[0] += 8

    def cols(sem, buf, land, rsem):
        at = 32 * s
        go(sem, [RemoteDMATransfer(dst_ids=[dest(topo, core, d)], dma_engine_mask=eng(topo, core, d, 4 * i, 4 * i + 4), remote_sem=T.sem[rsem],
                                   src=view(T, buf, 32 * i, 32 * i + 32), dst=view(T, land, at, at + 32)) for i, d in enumerate(to)])

    def note(sem, src, land, rsem):
        go(sem, [RemoteDMATransfer(dst_ids=[dest(topo, core, d) for d in to], dma_engine_mask=eng(topo, core, to[0], 0, 8), remote_sem=T.sem[rsem],
                                   srcs=[T[src][:]], dsts=[T[land][:, 8 * s:8 * s + 1]] * 2)])

    note("rn1", "rm1", "nl1", "n1")
    cols("rc1", "r1c", "land1c", "a1")
    cols("rs1", "r1s", "land1s", "a1")
    note("rn2", "rm2", "cl", "c2")
    cols("rc3", "r3c", "land3c", "a3")
    cols("rs3", "r3s", "land3s", "a3")
    note("rn3", "rm3", "nl3", "n3")
    g.wait_ge(T.sem.ls, sent[0])


def rank_program(g, core, T, topo):
    same_all, cross_all, relays_all = wiring(T, topo)
    me = T.rank_of(core)
    if me is None:
        for s in range(N):
            if core in relays_all[s]:
                i = relays_all[s].index(core)
                relay_program(g, core, T, topo, s, cross_all[s][2 * i:2 * i + 2])
        return
    same, cross, relays = same_all[me], cross_all[me], relays_all[me]
    pos = cross + same
    am = same.index(me)
    peer = [r for r in same if r != me and T.cores[r] in topo.cores_of(core)]
    far = [r for r in same if r != me and r not in peer]
    ncol = 8 * len(peer) + 4 * len(far) + 4 * len(cross)
    nmsg = 8 * (N - 1)

    V, S, E, Y = g.vector, g.scalar, g.tensor, g.sync
    Q = {"v": V, "s": S, "t": E, "p": g, "y": Y}
    cnt, seen = {}, {}

    def wait(q, deps):
        best = {}
        for s, v in deps:
            best[s] = max(best.get(s, 0), v)
        for s, v in best.items():
            if seen.get((q, s), 0) < v:
                Q[q].wait_ge(T.sem[s], v)
                seen[(q, s)] = v

    def do(q, call, *deps):
        wait(q, deps)
        name = "q" + q
        cnt[name] = cnt.get(name, 0) + 1
        call().then_inc(T.sem[name], 1)
        return (name, cnt[name])

    def load(q, sem, out, in_, *deps):
        wait(q, deps)
        cnt[sem] = cnt.get(sem, 0) + 16
        Q[q].dma_start(out, in_).then_inc(T.sem[sem], 16)
        return (sem, cnt[sem])

    def vset(ap, c, *deps):
        return do("v", lambda: V.memset(ap, c), *deps)

    def ts(out, in0, s1, s2, op0, op1, *deps):
        if op1 is None:
            return do("v", lambda: V.tensor_scalar(out, in0, s1, None, op0), *deps)
        return do("v", lambda: V.tensor_scalar(out, in0, s1, s2, op0, op1), *deps)

    def tt(out, a, b, op, *deps):
        return do("v", lambda: V.tensor_tensor(out, a, b, op), *deps)

    def vcopy(out, in_, *deps):
        return do("v", lambda: V.tensor_copy(out, in_), *deps)

    def red(out, in_, op, *deps):
        return do("v", lambda: V.tensor_reduce(out, in_, X, op), *deps)

    def scan(out, d0, d1, *deps, init=0.0, op1=OP.add):
        return do("v", lambda: V.tensor_tensor_scan(out, d0, d1, init, OP.mult, op1), *deps)

    def runs(out, in_, *deps):
        return do("v", lambda: V.tensor_tensor_scan(out, in_, in_, 0.0, OP.add, OP.max), *deps)

    def turn(out, in_, *deps):
        return do("v", lambda: V.transpose(out, in_), *deps)

    def act(out, in_, *deps):
        return do("s", lambda: S.activation(out, in_, COPY), *deps)

    def affine(out, in_, scale, bias, *deps):
        return do("s", lambda: S.activation(out, in_, IDENT, bias, scale), *deps)

    def count_s(out, junk, in_, bias, *deps):
        return do("s", lambda: S.activation(junk, in_, SIGN, bias, -1.0, accum_out=out), *deps)

    def iota(ap, pattern, base, cm=0, flag=True):
        last = ("qp", cnt.get("qp", 0))
        if flag:
            return do("p", lambda: g.iota(ap, pattern, base, cm, allow_small_or_imprecise_dtypes=True), last)
        return do("p", lambda: g.iota(ap, pattern, base, cm), last)

    def spread(ns, out, in_, half, *deps):
        for k in range(8):
            a, b = k // 2, k // 2 ^ k % 2
            if k * ns % 8 < ns:
                hs = act(out(b, a), in_(a), *deps)
            else:
                hv = vcopy(out(b, a), in_(a), *deps)
        return vcopy(half(1, 0), half(0, 0), hv, hs), act(half(0, 1), half(1, 1), hv, hs)

    def quad(t, a, *cols):
        return T[t][(slice(32 * a, 32 * a + 32),) + cols]

    def pickc(out, win, off, *deps):
        return do("v", lambda: V.tensor_copy(out.bitcast(dt.uint32), win.bitcast(dt.uint32).indirect(off)), *deps)

    def pick(dst, src, n, a, b, off, *deps):
        return (pickc(T[dst + "c"][:, a:b], T[src[0]][:, 0:n], off, *deps), act(T[dst + "s"][:, a:b], T[src[1]][:, 0:n].indirect(off), *deps))

    def send(tr, *deps):
        wait("p", deps)
        g.remote_dma_fused([t for t, n in tr], local_sem=T.sem.ls)
        cnt["ls"] = cnt.get("ls", 0) + sum(n for t, n in tr)

    def xfer(src, dst, to, ab, sem):
        return (RemoteDMATransfer(dst_ids=[dest(topo, core, c) for c in to], dma_engine_mask=eng(topo, core, to[0], ab[0], ab[1]),
                                  remote_sem=T.sem[sem], srcs=[src], dsts=[dst] * len(to)), ab[1] - ab[0])

    def send_cross(buf, rbuf, sem, *deps):
        send([xfer(view(T, buf, 64 * i, 64 * i + 64), view(T, rbuf, 0, 64), [k], HAND[i], sem) for i, k in enumerate(relays)], *deps)

    def send_same(buf, land, sem, *deps):
        tr, at = [], 32 * me
        for i, r in enumerate(far + peer):
            a = 32 * pos.index(r)
            tr.append(xfer(view(T, buf, a, a + 32), view(T, land, at, at + 32), [T.cores[r]], COL["peer" if r in peer else i], sem))
        send(tr, *deps)

    def note(src, land, sem, to, ab):
        return xfer(src, T[land][:, 8 * me:8 * me + 1], [T.cores[r] for r in to], ab, sem)

    def note_out(src, rbuf, rsem, *deps):
        send([xfer(src[:, 0:1], T[rbuf][:], relays, MSG["relay"], rsem)], *deps)

    def note_same(src, land, sem, *deps):
        send([note(src, land, sem, far, MSG["far"]), note(src, land, sem, peer, MSG["peer"])], *deps)

    ldp = load("y", "ldp", T.plh[:, 0:16], T.pl[:, 0:16])
    ldx = load("s", "ldx", T.xh[:, 0:512], T.x[:])
    ldw = load("y", "ldw", T.wh[:], T.w[:], ldx)
    i_of = iota(T.off[:], [[1, L], [0, 8]], 0)
    i_p = iota(T.pb[:, 0:1], [[1, 1]], 0, 1, False)
    i_rh = iota(T.rhc[:], [[16, 4]], 0)
    for a in range(4):
        i_dq = iota(quad("dq", a, slice(0, 2)), [[pos[4 + a] - pos[a], 2]], pos[a])
    iota(T.c128[:], [[128, 8]], 0)
    iota(T.ggc[:], [[128, 8]], me)
    iota(T.cp[:], [[128, 2]], 0, 1)
    iota(T.c32[:], [[128, 2], [0, 32]], 0, 1)
    i_cc = iota(T.ccr[:], [[-1, 256]], 255)
    c_pl = vset(T.plh[:, 16:512], 0.0)
    h = vset(T.rstb[:], 1.0)
    c_of = vcopy(T.ofp[:], T.off[:], i_of)
    c_x = vset(T.xh[:, 512:520], 0.0)
    ts(T.pb[:, 1:2], T.pb[:, 0:1], 15, None, OP.bitwise_and, None, i_p)
    ts(T.pb[:, 2:3], T.pb[:, 0:1], 4, 1, OP.logical_shift_right, OP.bitwise_and)
    h2 = ts(T.pb[:, 3:4], T.pb[:, 0:1], 5, None, OP.logical_shift_right, None)
    c_rb = vset(T.rstb[:, 0:384:3], 0.0, h)
    c_pb = vcopy(T.pbf[:], T.pb[:], h2)
    rho, p16, p32 = [T.pbf[:, i:i + 1] for i in (1, 2, 3)]
    c_rh = affine(T.rh[:], T.rhc[:], 1.0, rho, c_pb, i_rh)

    plq = do("v", lambda: V.quantize_mx(T.plc[:], T.pls[:], T.plh[:]), ldp, c_pl)
    pr = []
    for b in range(L):
        w, o = slice(128 * b, 128 * b + 128), slice(8 * b, 8 * b + 8)
        hv = pickc(T.prc[:, w], T.plc[:], T.ofp[:, o], plq, c_of)
        pr.append((hv, act(T.prs[:, w], T.pls[:].indirect(T.ofp[:, o]), plq, c_of)))
        if b == 0:
            xq = do("v", lambda: V.quantize_mx(T.xq[:], T.xs[:], T.xh[:]), ldx, c_x)
    ts(T.nx[:], p16, -1.0, 1.0, OP.mult, OP.add, c_pb)
    c_bi = ts(T.bi[:], T.rhc[:], rho, 0.5, OP.add, OP.add, i_rh)
    zs = [T.z0, T.z1, T.z2]
    for b in range(L):
        w = slice(128 * b, 128 * b + 128)
        z = do("t", lambda: E.matmul_mx(zs[b][:, 0:128], T.prc[:, w], T.prs[:, w], T.xq[:, 0:128], T.xs[:, 0:128], True, True), xq, *pr[b])
        h = ts(T.bits[:, b:384:3], zs[b][:, 0:128], 0.0, float(2 ** b), OP.is_lt, OP.mult, z)
    bs = scan(T.bs[:], T.rstb[:], T.bits[:], h, c_rb)

    XQ, L1, CC = ("xq", "xs"), ("land1c", "land1s"), ("ccc", "ccs")
    w2 = [slice(128 * e, 128 * e + 128) for e in range(2)]
    hm = [ts(T.mt[:, w], T.bs[:, 2:384:3], T.dq[:, e:e + 1], None, OP.is_equal, None, bs, i_dq) for e, w in enumerate(w2)]
    cu = [runs(T.cu[:, w], T.mt[:, w], hm[e]) for e, w in enumerate(w2)]
    hs = [count_s(T.acc1[:, e:e + 1], T.junk1[:, w], T.cu[:, w], T.bi[:, 1:2], cu[e], c_bi) for e, w in enumerate(w2)]
    hc = [ts(T.cm[:, w], T.cu[:, w], T.rh[:, 0:1], None, OP.is_le, None, cu[e], c_rh) for e, w in enumerate(w2)]
    h0 = [red(T.lq[:, e, 0:1], T.cm[:, w], OP.add, hc[e]) for e, w in enumerate(w2)]
    hl = ts(T.la1[:], T.lq[:, :, 0], T.nx[:, 0:1], None, OP.mult, None, *h0)
    for e in range(2):
        lq = ts(T.lq[:, e, 1:2], T.acc1[:, e:e + 1], 0.5, 64.0, OP.mult, OP.add, hs[e])
        m1 = affine(T.m1[:, e:e + 1], T.lq[:, e, 1:2], p16, T.la1[:, e:e + 1], lq, hl)
        if e == 0:
            note_out(T.m1, "rm1", "rn1", m1)
    la = spread(3, lambda b, a: quad("la", b, slice(0, 2), slice(2 * a, 2 * a + 2)), lambda a: quad("lq", a, slice(0, 2), slice(0, 2)),
                lambda b, a: T.la[64 * b:64 * b + 64, :, 4 * a:4 * a + 4], lq, *h0)
    o0 = vcopy(T.off1[:, 0:8], T.la[:, 0, :], *la)
    o1 = vcopy(T.off1[:, 8:16], T.la[:, 1, :])
    pc, ps = pick("slot1", XQ, 130, 0, 128, T.off1[:, 0:8], o0, xq)
    send_cross("slot1c", "r1c", "rc1", pc)
    send_cross("slot1s", "r1s", "rs1", ps)
    note_same(T.m1[:, 1:2], "nl1", "n1", m1)
    pc, ps = pick("slot1", XQ, 130, 128, 256, T.off1[:, 8:16], o1, xq)
    send_same("slot1c", "land1c", "a1", pc)
    send_same("slot1s", "land1s", "a1", ps)
    i = pos.index(me)
    own1 = pick("land1", XQ, 130, 32 * me, 32 * me + 32, T.off1[:, 2 * i:2 * i + 2], o1, xq)
    own_n = vcopy(T.nl1[:, 8 * me:8 * me + 1], T.m1[:, 1:2], m1)

    load("y", "ldz", T.land3c[:, 256:258].bitcast(dt.uint8), T.xq[:, 128:130].bitcast(dt.uint8), xq)
    ldz = load("y", "ldz", T.land3s[:, 256:258], T.xs[:, 128:130], xq)
    c_nb = vset(T.nb[:], 0.0)
    h = vset(T.dm0[:], 0.9375)
    c_dm = do("p", lambda: g.affine_select(T.dm[:], T.dm0[:], [[-1, 128]], OP.is_equal, 0.0, 0, 1), h, i_cc)
    for b in range(2):
        w = 128 + 128 * b
        c_tri = ts(T.tri[:, 128 * b:128 * b + w], T.ccr[:, 256 - w:256], T.cp[:, b:b + 1], BIG, OP.is_lt, OP.mult, i_cc)
    c_one = vset(T.one[:], 1.0)
    h = vset(T.rst2[:], 1.0)
    c_r2 = vset(T.rst2[:, 0:512:256], 0.0, h)
    h = vset(T.rst9[:], 1.0)
    vset(T.rst9[:, 0:72:9], 0.0, h)
    h = ts(T.k8[:, 0:1], p32, 64.0, rho, OP.mult, OP.add)
    h = ts(T.rq[:], T.rhc[:], T.k8[:, 0:1], None, OP.add, None, h)
    c_bq = ts(T.bq[:], T.rq[:], 0.5, None, OP.add, None, h)
    h = ts(T.k8[:, 0:1], rho, 8.0, None, OP.mult, None, c_bq)
    ts(T.k8[:, 1:2], T.k8[:, 0:1], 128.0, None, OP.add, None, h)
    c_gg = ts(T.gg[:], T.ggc[:], T.k8[:, 0:1], None, OP.add, None, h)
    vcopy(T.it[:, 0:72:9], T.gg[:], c_gg)
    for i in range(N):
        vset(T.rc[:, i:i + 1], 2048.0 + pos[i])
    ts(T.rc[:, 8:10], T.dq[:], 2048.0, None, OP.add, None)
    vset(T.nf[:], 0.0)
    vset(T.nft[:, 256:264], -1.0)
    c_all = do("v", lambda: V.quantize_mx(T.wq[:], T.ws[:], T.wh[:]), ldw)

    a1, n1 = ("a1", 2 * ncol), ("n1", nmsg)
    h = tt(T.nb[:, 0:256:32], T.nl1[:, 0:64:8], T.c128[:], OP.add, n1, own_n, c_nb, i_cc)
    nt = turn(T.nt[:], T.nb[:], h)
    n8 = do("p", lambda: g.partition_broadcast(T.n8[:], T.nl1[32 * am:32 * am + 1, 0:64:8], 128), n1, own_n, c_dm)
    nw = do("p", lambda: g.partition_broadcast(T.nw[:], T.nt[32 * am:32 * am + 1, :], 128), nt, n8)
    h = ts(T.em[:], T.n8[:], P - 1.0, None, OP.is_gt, None, n8)
    h = scan(T.ep[:], T.em[:], T.one[:, 0:8], h, c_one, init=32.0, op1=OP.mult)
    h = red(T.k0[:], T.ep[:], OP.add, h)
    ts(T.ab1[:], T.c32[:], T.k0[:, 0:1], -2 * BIG, OP.is_equal, OP.mult, h)
    h = ts(T.ab2[:], T.c32[:], T.k0[:, 0:1], 2 * BIG, OP.is_lt, OP.mult)
    ab = tt(T.ab[:], T.ab1[:], T.ab2[:], OP.add, h)

    gs, gm = [T.ga, T.gb], []
    wd = [(slice(128 * b, 128 * b + 128), slice(128 * b, 128 + 256 * b), 128 + 128 * b) for b in range(2)]
    for b in range(2):
        w, w2, n = wd[b]
        gm.append(do("t", lambda: E.matmul_mx(gs[b][:, 0:n], T.land1c[:, w], T.land1s[:, w], T.land1c[:, 0:n], T.land1s[:, 0:n], True, True), a1, *own1))
    mx, th, hl, tr = [], [], [], []
    for b in range(2):
        w, w2, n = wd[b]
        h = tt(T.pd[:, w], gs[b][:, w], T.dm[:], OP.mult, gm[b], c_dm)
        th.append(do("s", lambda: S.activation(T.junk2[:, w], T.pd[:, w], COPY, accum_out=T.thr[:, b:b + 1]), h))
        mx.append(do("v", lambda: V.tensor_tensor_scan(T.xg[:, w2], gs[b][:, n - 1::-1], T.tri[:, w2], 0.0, OP.max, OP.min), c_tri))
    for b in range(2):
        w = slice(32 * b, 32 * b + 32)
        at = 128 * b + wd[b][2] - 1
        hl.append(ts(T.tt[:, w], T.ab[:, w], T.xg[:, at:at + 1], T.thr[:, b:b + 1], OP.add, OP.is_lt, mx[b], th[b], ab))
    for b in range(2):
        tr.append(turn(T.tw[:, b, :], T.tt[:, 32 * b:32 * b + 32], hl[b]))
    bc = spread(4, lambda b, a: quad("bc", b, slice(0, 2), slice(32 * a, 32 * a + 32)), lambda a: quad("tw", a, slice(0, 2), slice(0, 32)),
                lambda b, a: T.bc[64 * b:64 * b + 64, :, 64 * a:64 * a + 64], *tr)
    h = scan(T.cum[:, 0:128], T.rst2[:, 1:129], T.bc[:, 0, :], *bc)
    cum = scan(T.cum[:, 128:256], T.rst2[:, 1:129], T.bc[:, 1, :], h, c_r2, init=T.cum[:, 127:128])

    size = T.cum[:, 255:256]
    send([xfer(size, T.rm2[:], [k], HAND[i], "rn2") for i, k in enumerate(relays)], cum)
    note_same(size, "cl", "c2")
    for c in range(2):
        w = slice(256 * c, 256 * c + 256)
        sa = count_s(T.acc2[:, c:c + 1], T.junk3[:, w], T.cum[:], T.bq[:, 2 + c:3 + c], cum, c_bq)
        h = ts(T.cm2[:, w], T.cum[:], T.rq[:, c:c + 1], None, OP.is_le, None, cum)
    h = scan(T.su2[:], T.rst2[:], T.cm2[:], h)
    vcopy(T.nq[:, 0:2], T.su2[:, 255:512:256], h)
    h = ts(T.nq[:, 2:4], T.acc2[:], 0.5, 128.0, OP.mult, OP.add, sa)
    na = spread(4, lambda b, a: quad("na", b, slice(4 * a, 4 * a + 4)), lambda a: quad("nq", a, slice(0, 4)),
                lambda b, a: T.na[64 * b:64 * b + 64, 8 * a:8 * a + 8], h)
    oc = ts(T.offc[:], T.na[:], 255.0, None, OP.min, None, *na)
    ck = pick("cc", L1, 256, 0, 256, T.offc[:], oc, a1, *own1)
    own_c = vcopy(T.cl[:, 8 * me:8 * me + 1], size)
    nwc = act(T.nwc[:], T.nw[:].indirect(T.offc[:]), oc, nw)

    end = scan(T.end[:], T.one[:, 0:8], T.cl[:, 0:64:8], ("c2", nmsg), own_c)
    h = ts(T.vi[:], T.rc[:], T.end[:, me - 1:me] if me else 0.0, None, OP.subtract, None, end)
    h = ts(T.v7[:], T.vi[:], 7, None, OP.bitwise_and, None, h)
    ts(T.off3[:, 0:20:2], T.v7[:], T.k8[:, 0:1], None, OP.add, None, h)
    o3 = ts(T.off3[:, 1:20:2], T.v7[:], T.k8[:, 1:2], None, OP.add, None)
    pc, ps = pick("slot3", CC, 256, 0, 128, T.off3[:, 0:8], o3, *ck)
    send_cross("slot3c", "r3c", "rc3", pc)
    send_cross("slot3s", "r3s", "rs3", ps)
    n3 = act(T.n3[:], T.nwc[:].indirect(T.off3[:, 16:20]), o3, nwc)
    pc, ps = pick("slot3", CC, 256, 128, 256, T.off3[:, 8:16], o3, *ck)
    h = turn(T.nt3[:], T.n3[:], n3)
    m3 = vcopy(T.m3[:], T.nt3[:, 0:64:32], h)
    own_n3 = vcopy(T.nl3[:, 8 * me:8 * me + 1], T.nt3[:, 32:33])
    note_out(T.m3, "rm3", "rn3", m3)
    send_same("slot3c", "land3c", "a3", pc)
    send_same("slot3s", "land3s", "a3", ps)
    note_same(T.m3[:, 1:2], "nl3", "n3", m3)
    i = pos.index(me)
    own3 = pick("land3", CC, 256, 32 * me, 32 * me + 32, T.off3[:, 2 * i:2 * i + 2], o3, *ck)

    h = ts(T.d256[:], T.cl[:, 0:64:8], -1.0, 256.0, OP.mult, OP.add)
    for d in range(N):
        h2 = ts(T.it[:, 1 + d:72:9], T.gg[:], T.end[:, d:d + 1], T.d256[:, d:d + 1], OP.is_ge, OP.mult, h)
    h = scan(T.its[:], T.rst9[:], T.it[:], h2)
    h = vcopy(T.xi[:], T.its[:, 8:72:9], h)
    h = ts(T.xsh[:], T.xi[:], 3, None, OP.logical_shift_right, None, h)
    oz = ts(T.offz[:], T.xsh[:], 256.0, None, OP.min, None, h)

    a3 = ("a3", 2 * ncol)
    fc = pickc(T.fq[:], T.land3c[:], T.offz[:], a3, ldz, oz, *own3)
    fs = act(T.fs[:], T.land3s[:].indirect(T.offz[:]), a3, ldz, oz, *own3)
    yp = do("t", lambda: E.matmul_mx(T.yp[:, 0:128], T.wq[:], T.ws[:], T.fq[:], T.fs[:], True, True), fc, fs, c_all)
    load("y", "dout", T.oc[:], T.fq[:].bitcast(dt.uint8), fc)
    h = vcopy(T.nf[:, 0:256:32], T.nl3[:, 0:64:8], ("n3", nmsg), own_n3)
    h = turn(T.nft[:, 0:256], T.nf[:], h)
    no = do("v", lambda: V.tensor_copy(T.no[:], T.nft[:].indirect(T.offz[:])), h)
    for k in range(4):
        load("y", "dout", T.osc[4 * k:4 * k + 4, :], T.fs[32 * k:32 * k + 4, :], fs)
    ys = act(T.ysb[:], T.yp[:, 0:128], yp)
    load("s", "dout", T.y[:], T.ysb[:], ys)
    load("y", "dout", T.num[:], T.no[32 * am:32 * am + 1, :], no)
    wait("p", [(s, cnt[s]) for s in ("qv", "qs", "qt", "qp", "dout", "ls", "ldz", "ldp", "ldx", "ldw")])
